import numpy as np
import ml_dtypes


def mxq(x, axis, fmt="e4m3"):
    dtype, down = {"e4m3": (ml_dtypes.float8_e4m3fn, 7), "e5m2": (ml_dtypes.float8_e5m2, 14)}[fmt]
    v = np.moveaxis(np.asarray(x, np.float32).astype(ml_dtypes.bfloat16).astype(np.float64), axis, -1)
    blocks = v.reshape(v.shape[:-1] + (-1, 32))
    amax = np.abs(blocks).max(-1, keepdims=True)
    byte = np.maximum(np.where(amax > 0, np.frexp(amax)[1] - 1 + 127, 0) - down, 1)
    scale = np.exp2(byte - 127.0)
    codes = (blocks / scale).astype(np.float32).astype(dtype).astype(np.float64)
    return np.moveaxis((codes * scale).reshape(v.shape), -1, axis)


WIDE = False


def mx_kscale(k):
    if not WIDE:
        return np.ones(k)
    levels = np.array([30, -30])
    if k % 512:
        return np.exp2(np.random.permutation(np.resize(levels, k // 32))).repeat(32)
    a = np.empty((k // 512, 16))
    for p in range(k // 512):
        a[p, :8] = np.random.permutation(np.resize(levels, 8))
        for g in range(8):
            far = levels[np.abs(levels - a[p, g]) >= 10]
            a[p, g + 8] = far[np.random.randint(len(far))]
    return np.exp2(a.ravel()).repeat(32)


def f64(x):
    return np.asarray(x).astype(np.float64)


def striped(idx):
    return np.tile(idx.reshape(-1, 16).T, (8, 1)).astype(np.uint16)


def unstriped(offs):
    return offs[:16].T.reshape(-1).astype(np.int64)


E2M1 = np.array([0.0, 0.5, 1.0, 1.5, 2.0, 3.0, 4.0, 6.0, -0.0, -0.5, -1.0, -1.5, -2.0, -3.0, -4.0, -6.0])


def pack_weight(w, fmt):
    k, n = w.shape
    w = f64(np.asarray(w, np.float32).astype(ml_dtypes.bfloat16)).reshape(k // 32, 32, n)
    amax = np.abs(w).max(1)
    if fmt == "e4m3":
        byte = np.frexp(amax)[1] - 1 + 127 - 7
    else:
        mant, ex = np.frexp(amax / 6.0)
        byte = np.where(mant > 0.5, ex, ex - 1) + 127
    byte = np.clip(np.where(amax > 0, byte, 1), 1, 254)
    scaled = (w * np.exp2(127.0 - byte)[:, None, :]).reshape(k, n).astype(np.float32)
    by_word = np.ascontiguousarray(scaled.reshape(k // 512, 128, 4, n).transpose(0, 1, 3, 2))
    if fmt == "e4m3":
        words = by_word.astype(ml_dtypes.float8_e4m3fn).view(np.uint8)
    else:
        c = by_word.astype(ml_dtypes.float4_e2m1fn).view(np.uint8) & 0xF
        words = (c[..., 0::2] | (c[..., 1::2] << 4)).reshape(k // 512, 128, 2 * n)
    return np.ascontiguousarray(words), np.ascontiguousarray(byte.astype(np.uint8).reshape(k // 512, 16, n))


def unpack_weight(words, scales, fmt):
    g, _, n = scales.shape
    words = np.ascontiguousarray(words).reshape(g, 128, n, -1)
    if fmt == "e4m3":
        vals = words.view(ml_dtypes.float8_e4m3fn).astype(np.float64)
    else:
        nib = np.empty((g, 128, n, 4), np.uint8)
        nib[..., 0::2] = words & 0xF
        nib[..., 1::2] = words >> 4
        vals = E2M1[nib]
    vals = vals * np.repeat(np.exp2(scales.astype(np.float64) - 127.0), 8, axis=1)[..., None]
    return vals.transpose(0, 1, 3, 2).reshape(g * 512, n)


K, N, T, J = 512, 512, 2048, 1024


def setup_inputs():
    n = np.random.standard_normal
    s = mx_kscale(K)[:, None]
    m = np.exp(0.5 * n((1, J)))
    w = n((K, N)) / np.sqrt(K) / s
    w4 = pack_weight(w, "e2m1")
    wrest = w - unpack_weight(*w4, "e2m1")
    p_w8 = pack_weight(wrest, "e4m3")
    return {
        "dy": (m * n((K, J)) * s).astype(np.float32),
        "w4_words": w4[0],
        "w4_scales": w4[1],
        "w8_words": p_w8[0],
        "w8_scales": p_w8[1],
        "wgo": np.tile(np.random.uniform(0.5, 2.0, J), (128, 1)).astype(np.float32),
        "offs": striped(np.random.permutation(T)[:J]),
    }


def reference(dy, w4_words, w4_scales, w8_words, w8_scales, wgo, offs):
    idx = unstriped(offs)
    dy_ = mxq(f64(dy), 0, "e5m2")
    w4_ = unpack_weight(w4_words, w4_scales, "e2m1")
    w8_ = unpack_weight(w8_words, w8_scales, "e4m3")
    dx = w4_.T @ dy_ + w8_.T @ dy_
    out = np.zeros((N, T))
    out[:, idx] = f64(wgo)[0] * (dx)
    return out

@@ -1,0 +1,116 @@
+import concourse.mybir as mybir
+
+K, N, T, J = 512, 512, 2048, 1024
+FLOPS = 2 * 2 * K * N * J
+
+F32 = mybir.dt.float32
+BF16 = mybir.dt.bfloat16
+I32 = mybir.dt.int32
+U32 = mybir.dt.uint32
+U16 = mybir.dt.uint16
+U8 = mybir.dt.uint8
+E5M2 = mybir.dt.float8_e5m2_x4
+E4M3 = mybir.dt.float8_e4m3fn_x4
+E2M1 = mybir.dt.float4_e2m1fn_x4
+
+P = 128
+HALF = 512
+
+
+def tile_list_embg_res_none_kernel(tc, dy, w4_words, w4_scales, w8_words, w8_scales, wgo, offs, out):
+    nc = tc.nc
+    mult = mybir.AluOpType.mult
+    dy_rows = dy.rearrange("(p t) j -> p t j", t=4)
+
+    with tc.tile_pool(name="keep", bufs=1) as keep, tc.psum_pool(name="psum", bufs=1) as psum:
+        offsets = keep.tile([P, J // 16], U16, name="offsets")
+        w4 = keep.tile([P, 2 * N], U8, name="w4", align_bytes=64)
+        w8 = keep.tile([P, N], U32, name="w8", align_bytes=64)
+        s4 = keep.tile([P, N], U8, name="s4", align_bytes=64)
+        s8 = keep.tile([P, N], U8, name="s8", align_bytes=64)
+        gain = keep.tile([P, J], F32, name="gain")
+        codes = [keep.tile([P, HALF], U32, name="codes0", align_bytes=64)]
+        scales = [keep.tile([P, HALF], U8, name=f"scales{h}", align_bytes=64) for h in range(2)]
+        pages = [keep.tile([P, T], F32, name=f"page{w}", align_bytes=64) for w in range(2)]
+        pieces = [(0, 256), (256, 384), (384, 512), (512, 768), (768, 1024)]
+        raw = [keep.tile([P, 4, b - a], F32, name=f"raw{a}", tag=f"raw{a}") for a, b in pieces]
+        woven = [keep.tile([P, b - a, 4], BF16, name=f"woven{a}", tag=f"woven{a}", align_bytes=64)[:] for a, b in pieces[:3]]
+        woven_late = keep.tile([P, HALF, 4], BF16, name="woven_late", align_bytes=64)
+        woven.extend([woven_late[:, :256, :], woven_late[:, 256:, :]])
+
+        def load_scales(plane, rows):
+            for q in range(4):
+                quad = rows[0, 4 * q : 4 * q + 4, :].bitcast(I32)
+                nc.scalar.dma_start(plane[32 * q : 32 * q + 32, :].bitcast(I32), quad.partition_broadcast(8))
+
+        def load_dy(i):
+            a, b = pieces[i]
+            nc.sync.dma_start(raw[i][:], dy_rows[:, :, a:b])
+
+        def weave(copy, i):
+            copy(out=woven[i].rearrange("p (c i) t -> p c t i", i=2),
+                 in_=raw[i][:].rearrange("p t (c i) -> p c t i", i=2))
+
+        def quantise(h, a, b, source):
+            nc.vector.quantize_mx(out=codes[h][:, a:b].bitcast(E5M2), scales=scales[h][:, a:b],
+                                  in_=source.rearrange("p c t -> p (c t)"))
+
+        def product(nb, h):
+            acc = psum.tile([P, HALF], F32, name=f"acc{nb}{h}")
+            cols = slice(nb * P, (nb + 1) * P)
+            nc.tensor.matmul_mx(out=acc[:], lhsT=w4[:, 2 * nb * P : 2 * (nb + 1) * P].bitcast(E2M1), lhsT_scale=s4[:, cols],
+                                rhs=codes[h][:].bitcast(E5M2), rhs_scale=scales[h][:], start=True, stop=False)
+            nc.tensor.matmul_mx(out=acc[:], lhsT=w8[:, cols].bitcast(E4M3), lhsT_scale=s8[:, cols],
+                                rhs=codes[h][:].bitcast(E5M2), rhs_scale=scales[h][:], start=False, stop=True)
+            return acc
+
+        def scatter(page, dx, a, b):
+            nc.vector.tensor_tensor(out=page[:].indirect(offsets[:, a // 16 : b // 16]), in0=dx, in1=gain[:, a:b], op=mult)
+
+        def store(nb, page):
+            nc.sync.dma_start(out[nb * P : (nb + 1) * P, :], page[:])
+
+        load_scales(s4, w4_scales)
+        load_scales(s8, w8_scales)
+        for i in range(3):
+            load_dy(i)
+        nc.sync.dma_start(w4[:].bitcast(I32), w4_words[0].bitcast(I32))
+        nc.sync.dma_start(w8[:].bitcast(I32), w8_words[0].rearrange("p n t -> p (n t)").bitcast(I32))
+        nc.sync.dma_start(gain[:, :HALF], wgo[:, :HALF])
+        nc.sync.dma_start(offsets[:], offs)
+        load_dy(3)
+        load_dy(4)
+        nc.sync.dma_start(gain[:, HALF:], wgo[:, HALF:])
+
+        for page in pages:
+            nc.vector.memset(page[:].bitcast(I32), 0)
+        for i in range(3):
+            weave(nc.vector.tensor_copy, i)
+            quantise(0, *pieces[i], woven[i])
+        third = keep.tile([P, T], F32, name="third", tag="woven384", align_bytes=64)
+        nc.vector.memset(third[:].bitcast(I32), 0)
+        pages.append(third)
+
+        first = [product(nb, 0) for nb in range(4)]
+        for nb in range(2):
+            dx = keep.tile([P, HALF], F32, name=f"dx{nb}0", tag=f"dx{nb}0", align_bytes=64)
+            (nc.scalar.copy if nb else nc.vector.tensor_copy)(out=dx[:], in_=first[nb][:])
+            scatter(pages[nb], dx[:], 0, HALF)
+        weave(nc.scalar.copy, 3)
+        weave(nc.scalar.copy, 4)
+        codes.append(keep.tile([P, HALF], U32, name="codes1", tag="dx00", align_bytes=64))
+        quantise(1, 0, HALF, woven_late[:])
+        dx = keep.tile([P, HALF], F32, name="dx20", tag="raw768")
+        nc.scalar.copy(out=dx[:], in_=first[2][:])
+        scatter(pages[2], dx[:], 0, HALF)
+        second = [product(nb, 1) for nb in range(4)]
+        for nb in range(3):
+            dx = keep.tile([P, HALF], F32, name=f"dx{nb}1")
+            nc.scalar.copy(out=dx[:], in_=second[nb][:])
+            scatter(pages[nb], dx[:], HALF, J)
+            store(nb, pages[nb])
+        dx = keep.tile([P, J], F32, name="dx3")
+        nc.scalar.copy(out=dx[:, :HALF], in_=first[3][:])
+        nc.scalar.copy(out=dx[:, HALF:], in_=second[3][:])
+        scatter(pages[0], dx[:], 0, J)
+        store(3, pages[0])

@@ -38,10 +38,9 @@ def tile_list_embg_res_none_kernel(tc, dy, w4_words, w4_scales, w8_words, w8_sca
         woven_late = keep.tile([P, HALF, 4], BF16, name="woven_late", align_bytes=64)
         woven.extend([woven_late[:, :256, :], woven_late[:, 256:, :]])
 
-        def load_scales(plane, rows):
-            for q in range(4):
-                quad = rows[0, 4 * q : 4 * q + 4, :].bitcast(I32)
-                nc.scalar.dma_start(plane[32 * q : 32 * q + 32, :].bitcast(I32), quad.partition_broadcast(8))
+        def load_scales(queue, plane, rows, q):
+            quad = rows[0, 4 * q : 4 * q + 4, :].bitcast(I32)
+            queue.dma_start(plane[32 * q : 32 * q + 32, :].bitcast(I32), quad.partition_broadcast(8))
 
         def load_dy(i):
             a, b = pieces[i]
@@ -70,8 +69,10 @@ def tile_list_embg_res_none_kernel(tc, dy, w4_words, w4_scales, w8_words, w8_sca
         def store(nb, page):
             nc.sync.dma_start(out[nb * P : (nb + 1) * P, :], page[:])
 
-        load_scales(s4, w4_scales)
-        load_scales(s8, w8_scales)
+        for q in range(4):
+            load_scales(nc.sync if q < 2 else nc.scalar, s4, w4_scales, q)
+        for q in range(4):
+            load_scales(nc.scalar, s8, w8_scales, q)
         for i in range(3):
             load_dy(i)
         nc.sync.dma_start(w4[:].bitcast(I32), w4_words[0].bitcast(I32))
@@ -82,14 +83,14 @@ def tile_list_embg_res_none_kernel(tc, dy, w4_words, w4_scales, w8_words, w8_sca
         load_dy(4)
         nc.sync.dma_start(gain[:, HALF:], wgo[:, HALF:])
 
-        for page in pages:
-            nc.vector.memset(page[:].bitcast(I32), 0)
+        nc.vector.memset(pages[0][:].bitcast(I32), 0)
+        nc.gpsimd.memset(pages[1][:], 0.0)
         for i in range(3):
             weave(nc.vector.tensor_copy, i)
             quantise(0, *pieces[i], woven[i])
         third = keep.tile([P, T], F32, name="third", tag="woven384", align_bytes=64)
         nc.vector.memset(third[:].bitcast(I32), 0)
-        pages.append(third)
+        pages.insert(1, third)
 
         first = [product(nb, 0) for nb in range(4)]
         for nb in range(2):

@@ -1,4 +1,5 @@
 import concourse.mybir as mybir
+from concourse.masks import make_identity
 
 K, N, T, J = 512, 512, 2048, 1024
 FLOPS = 2 * 2 * K * N * J
@@ -15,103 +16,165 @@ E2M1 = mybir.dt.float4_e2m1fn_x4
 
 P = 128
 HALF = 512
+PAGE_BYTES = 4 * T
+WOVEN_BYTES = 2 * 4 * P
+EARLY = 3 * P
+LATE_AT = 2 * PAGE_BYTES + WOVEN_BYTES
 
 
 def tile_list_embg_res_none_kernel(tc, dy, w4_words, w4_scales, w8_words, w8_scales, wgo, offs, out):
     nc = tc.nc
-    mult = mybir.AluOpType.mult
+    mult, add = mybir.AluOpType.mult, mybir.AluOpType.add
+    copy_fn = mybir.ActivationFunctionType.Copy
     dy_rows = dy.rearrange("(p t) j -> p t j", t=4)
 
-    with tc.tile_pool(name="keep", bufs=1) as keep, tc.psum_pool(name="psum", bufs=1) as psum:
+    with (
+        tc.tile_pool(name="keep", bufs=1) as keep,
+        tc.tile_pool(name="chain", bufs=1) as chain,
+        tc.psum_pool(name="psum", bufs=1) as psum,
+    ):
         offsets = keep.tile([P, J // 16], U16, name="offsets")
         w4 = keep.tile([P, 2 * N], U8, name="w4", align_bytes=64)
         w8 = keep.tile([P, N], U32, name="w8", align_bytes=64)
         s4 = keep.tile([P, N], U8, name="s4", align_bytes=64)
         s8 = keep.tile([P, N], U8, name="s8", align_bytes=64)
-        gain = keep.tile([P, J], F32, name="gain")
-        codes = [keep.tile([P, HALF], U32, name="codes0", align_bytes=64)]
-        scales = [keep.tile([P, HALF], U8, name=f"scales{h}", align_bytes=64) for h in range(2)]
-        pages = [keep.tile([P, T], F32, name=f"page{w}", align_bytes=64) for w in range(2)]
-        pieces = [(0, 256), (256, 384), (384, 512), (512, 768), (768, 1024)]
-        raw = [keep.tile([P, 4, b - a], F32, name=f"raw{a}", tag=f"raw{a}") for a, b in pieces]
-        woven = [keep.tile([P, b - a, 4], BF16, name=f"woven{a}", tag=f"woven{a}", align_bytes=64)[:] for a, b in pieces[:3]]
-        woven_late = keep.tile([P, HALF, 4], BF16, name="woven_late", align_bytes=64)
-        woven.extend([woven_late[:, :256, :], woven_late[:, 256:, :]])
+        gain_col = keep.tile([P, 3], F32, name="gain_col")
+        gain = keep.tile([P, J - EARLY], F32, name="gain")
+        ident = keep.tile([P, P], F32, name="ident")
+        zeros = keep.tile([P, P], F32, name="zeros")
+        raw = [keep.tile([P, 4, P], F32, name=f"raw{b}", tag=f"raw{b}") for b in range(4)]
+        raw_late = chain.tile([P, 4, HALF], F32, name="raw_late", align_bytes=64, offset=LATE_AT)
+        pages = [keep.tile([P, T], F32, name=f"page{w}") for w in range(2)]
 
-        def load_scales(queue, plane, rows, q):
+        def load_scales(plane, rows, q):
             quad = rows[0, 4 * q : 4 * q + 4, :].bitcast(I32)
-            queue.dma_start(plane[32 * q : 32 * q + 32, :].bitcast(I32), quad.partition_broadcast(8))
+            nc.sync.dma_start(plane[32 * q : 32 * q + 32, :].bitcast(I32), quad.partition_broadcast(8))
 
-        def load_dy(i):
-            a, b = pieces[i]
-            nc.sync.dma_start(raw[i][:], dy_rows[:, :, a:b])
+        def weave(copy, woven, source):
+            copy(out=woven[:].rearrange("p (c i) t -> p c t i", i=2), in_=source[:].rearrange("p t (c i) -> p c t i", i=2))
 
-        def weave(copy, i):
-            copy(out=woven[i].rearrange("p (c i) t -> p c t i", i=2),
-                 in_=raw[i][:].rearrange("p t (c i) -> p c t i", i=2))
+        def quantise(woven, width, name):
+            codes = keep.tile([P, width], U32, name=f"codes_{name}", align_bytes=64)
+            scales = keep.tile([P, width], U8, name=f"scales_{name}", align_bytes=64)
+            nc.vector.quantize_mx(out=codes[:].bitcast(E5M2), scales=scales[:], in_=woven[:].rearrange("p c t -> p (c t)"))
+            return codes, scales
 
-        def quantise(h, a, b, source):
-            nc.vector.quantize_mx(out=codes[h][:, a:b].bitcast(E5M2), scales=scales[h][:, a:b],
-                                  in_=source.rearrange("p c t -> p (c t)"))
-
-        def product(nb, h):
-            acc = psum.tile([P, HALF], F32, name=f"acc{nb}{h}")
-            cols = slice(nb * P, (nb + 1) * P)
-            nc.tensor.matmul_mx(out=acc[:], lhsT=w4[:, 2 * nb * P : 2 * (nb + 1) * P].bitcast(E2M1), lhsT_scale=s4[:, cols],
-                                rhs=codes[h][:].bitcast(E5M2), rhs_scale=scales[h][:], start=True, stop=False)
-            nc.tensor.matmul_mx(out=acc[:], lhsT=w8[:, cols].bitcast(E4M3), lhsT_scale=s8[:, cols],
-                                rhs=codes[h][:].bitcast(E5M2), rhs_scale=scales[h][:], start=False, stop=True)
+        def product_by_token(b, codes, scales):
+            acc = psum.tile([P, N], F32, name=f"tok{b}", tag=("acc0", "acc0", "turn0", "acc3")[b])
+            nc.tensor.matmul_mx(out=acc[:], lhsT=codes[:].bitcast(E5M2), lhsT_scale=scales[:],
+                                rhs=w4[:].bitcast(E2M1), rhs_scale=s4[:], start=True, stop=False)
+            nc.tensor.matmul_mx(out=acc[:], lhsT=codes[:].bitcast(E5M2), lhsT_scale=scales[:],
+                                rhs=w8[:].bitcast(E4M3), rhs_scale=s8[:], start=False, stop=True)
             return acc
 
-        def scatter(page, dx, a, b):
-            nc.vector.tensor_tensor(out=page[:].indirect(offsets[:, a // 16 : b // 16]), in0=dx, in1=gain[:, a:b], op=mult)
+        def product_by_row(nb, codes, scales):
+            acc = psum.tile([P, HALF], F32, name=f"row{nb}", tag=f"acc{nb}")
+            cols = slice(nb * P, (nb + 1) * P)
+            nc.tensor.matmul_mx(out=acc[:], lhsT=w4[:, 2 * nb * P : 2 * (nb + 1) * P].bitcast(E2M1), lhsT_scale=s4[:, cols],
+                                rhs=codes[:].bitcast(E5M2), rhs_scale=scales[:], start=True, stop=False)
+            nc.tensor.matmul_mx(out=acc[:], lhsT=w8[:, cols].bitcast(E4M3), lhsT_scale=s8[:, cols],
+                                rhs=codes[:].bitcast(E5M2), rhs_scale=scales[:], start=False, stop=True)
+            return acc
 
-        def store(nb, page):
-            nc.sync.dma_start(out[nb * P : (nb + 1) * P, :], page[:])
+        def turn(sources, name, bank):
+            turned = psum.tile([P, len(sources), P], F32, name=f"turned_{name}", tag=bank)
+            for i, source in enumerate(sources):
+                nc.tensor.transpose(turned[:, i, :], source, ident[:])
+            return turned
 
-        for q in range(4):
-            load_scales(nc.sync if q < 2 else nc.scalar, s4, w4_scales, q)
-        for q in range(4):
-            load_scales(nc.scalar, s8, w8_scales, q)
-        for i in range(3):
-            load_dy(i)
+        def empty(bank, name, tag=None):
+            dx = keep.tile(list(bank.shape), F32, name=f"dx_{name}", tag=tag or f"dx_{name}")
+            nc.scalar.copy(out=dx[:], in_=bank)
+            return dx
+
+        def scatter(nb, dx, a, b):
+            window = pages[nb][:].indirect(offsets[:, a // 16 : b // 16])
+            if a < EARLY:
+                nc.vector.tensor_tensor(out=window, in0=dx, in1=zeros[:], op=add)
+            else:
+                nc.vector.tensor_tensor(out=window, in0=dx, in1=gain[:, a - EARLY : b - EARLY], op=mult)
+
+        for q in range(3):
+            load_scales(s4, w4_scales, q)
+        nc.sync.dma_start(raw[0][:], dy_rows[:, :, :P])
+        load_scales(s4, w4_scales, 3)
+        for q in range(3):
+            load_scales(s8, w8_scales, q)
         nc.sync.dma_start(w4[:].bitcast(I32), w4_words[0].bitcast(I32))
+        load_scales(s8, w8_scales, 3)
         nc.sync.dma_start(w8[:].bitcast(I32), w8_words[0].rearrange("p n t -> p (n t)").bitcast(I32))
-        nc.sync.dma_start(gain[:, :HALF], wgo[:, :HALF])
+        with nc.allow_non_contiguous_dma(reason="one weight a partition"):
+            nc.sync.dma_start(gain_col[:], wgo[0, :EARLY].rearrange("(b p) -> p b", p=P))
+        nc.sync.dma_start(raw[1][:], dy_rows[:, :, P : 2 * P])
         nc.sync.dma_start(offsets[:], offs)
-        load_dy(3)
-        load_dy(4)
-        nc.sync.dma_start(gain[:, HALF:], wgo[:, HALF:])
+        for b in (2, 3):
+            nc.sync.dma_start(raw[b][:], dy_rows[:, :, b * P : (b + 1) * P])
+        nc.sync.dma_start(raw_late[:], dy_rows[:, :, HALF:])
+        nc.sync.dma_start(gain[:], wgo[:, EARLY:])
 
-        nc.vector.memset(pages[0][:].bitcast(I32), 0)
-        nc.gpsimd.memset(pages[1][:], 0.0)
-        for i in range(3):
-            weave(nc.vector.tensor_copy, i)
-            quantise(0, *pieces[i], woven[i])
-        third = keep.tile([P, T], F32, name="third", tag="woven384", align_bytes=64)
-        nc.vector.memset(third[:].bitcast(I32), 0)
-        pages.insert(1, third)
+        make_identity(nc, ident[:])
+        nc.scalar.activation(out=zeros[:], in_=ident[:], func=copy_fn, scale=0.0)
+        for page in pages:
+            nc.vector.memset(page[:].bitcast(I32), 0)
 
-        first = [product(nb, 0) for nb in range(4)]
-        for nb in range(2):
-            dx = keep.tile([P, HALF], F32, name=f"dx{nb}0", tag=f"dx{nb}0", align_bytes=64)
-            (nc.scalar.copy if nb else nc.vector.tensor_copy)(out=dx[:], in_=first[nb][:])
-            scatter(pages[nb], dx[:], 0, HALF)
-        weave(nc.scalar.copy, 3)
-        weave(nc.scalar.copy, 4)
-        codes.append(keep.tile([P, HALF], U32, name="codes1", tag="dx00", align_bytes=64))
-        quantise(1, 0, HALF, woven_late[:])
-        dx = keep.tile([P, HALF], F32, name="dx20", tag="raw768")
-        nc.scalar.copy(out=dx[:], in_=first[2][:])
-        scatter(pages[2], dx[:], 0, HALF)
-        second = [product(nb, 1) for nb in range(4)]
-        for nb in range(3):
-            dx = keep.tile([P, HALF], F32, name=f"dx{nb}1")
-            nc.scalar.copy(out=dx[:], in_=second[nb][:])
-            scatter(pages[nb], dx[:], HALF, J)
-            store(nb, pages[nb])
-        dx = keep.tile([P, J], F32, name="dx3")
-        nc.scalar.copy(out=dx[:, :HALF], in_=first[3][:])
-        nc.scalar.copy(out=dx[:, HALF:], in_=second[3][:])
-        scatter(pages[0], dx[:], 0, J)
-        store(3, pages[0])
+        step = WOVEN_BYTES // 2
+        woven = chain.tile([P, P, 4], BF16, name="woven0", align_bytes=64, offset=PAGE_BYTES - step)
+        weave(nc.vector.tensor_copy, woven, raw[0])
+        blocks = [quantise(woven, P, "b0")]
+        pages.append(chain.tile([P, T], F32, name="page2", align_bytes=64, offset=0))
+        nc.vector.memset(pages[2][:].bitcast(I32), 0)
+        for b in (1, 2):
+            woven = chain.tile([P, P, 4], BF16, name=f"woven{b}", align_bytes=64, offset=PAGE_BYTES + (b - 1) * step)
+            weave(nc.vector.tensor_copy, woven, raw[b])
+            blocks.append(quantise(woven, P, f"b{b}"))
+        pages.append(chain.tile([P, T], F32, name="page3", align_bytes=64, offset=PAGE_BYTES + 2 * step))
+        nc.gpsimd.memset(pages[3][:], 0.0)
+
+        acc = product_by_token(0, *blocks[0])
+        by_token = keep.tile([P, N], F32, name="by_token0", tag="by_token0", align_bytes=64)
+        nc.scalar.activation(out=by_token[:, :P], in_=acc[:, :P], func=copy_fn, scale=gain_col[:, 0:1])
+        head = turn([by_token[:, :P]], "head", "turn0")
+        nc.scalar.activation(out=by_token[:, P:], in_=acc[:, P:], func=copy_fn, scale=gain_col[:, 0:1])
+        scatter(0, empty(head[:], "head")[:, 0, :], 0, P)
+        rest = turn([by_token[:, nb * P : (nb + 1) * P] for nb in (1, 2, 3)], "rest", "turn1")
+        dx = empty(rest[:], "rest")
+        for nb in (1, 2, 3):
+            scatter(nb, dx[:, nb - 1, :], 0, P)
+
+        def turned_block(b, bank):
+            acc = product_by_token(b, *blocks[b])
+            if b * P < EARLY:
+                by_token = keep.tile([P, N], F32, name=f"by_token{b}", tag=f"by_token{b}", align_bytes=64)
+                nc.scalar.activation(out=by_token[:], in_=acc[:], func=copy_fn, scale=gain_col[:, b : b + 1])
+            else:
+                by_token = chain.tile([P, N], F32, name=f"by_token{b}", align_bytes=64, offset=LATE_AT + 4 * N)
+                nc.scalar.copy(out=by_token[:], in_=acc[:])
+            return turn([by_token[:, nb * P : (nb + 1) * P] for nb in range(4)], f"b{b}", bank)
+
+        turned1 = turned_block(1, "turn2")
+        dx = empty(turned1[:, :2, :], "b1_low")
+        for nb in (0, 1):
+            scatter(nb, dx[:, nb, :], P, 2 * P)
+        turned2 = turned_block(2, "turn0")
+        woven = keep.tile([P, P, 4], BF16, name="woven3", tag="by_token1", align_bytes=64)
+        weave(nc.scalar.copy, woven, raw[3])
+        blocks.append(quantise(woven, P, "b3"))
+        dx = empty(turned1[:, 2:, :], "b1_high", "raw3")
+        for nb in (2, 3):
+            scatter(nb, dx[:, nb - 2, :], P, 2 * P)
+
+        woven = keep.tile([P, HALF, 4], BF16, name="woven_late", tag="by_token2", align_bytes=64)
+        weave(nc.scalar.copy, woven, raw_late)
+        late = quantise(woven, HALF, "late")
+        dx = chain.tile([P, 4, P], F32, name="dx_b2", align_bytes=64, offset=LATE_AT)
+        nc.scalar.copy(out=dx[:], in_=turned2[:])
+        for nb in range(4):
+            scatter(nb, dx[:, nb, :], 2 * P, EARLY)
+
+        turned3 = turned_block(3, "turn1")
+        for nb in range(4):
+            tail = keep.tile([P, J - EARLY], F32, name=f"tail{nb}")
+            nc.scalar.copy(out=tail[:, :P], in_=turned3[:, nb, :])
+            nc.scalar.copy(out=tail[:, P:], in_=product_by_row(nb, *late)[:])
+            scatter(nb, tail[:], EARLY, J)
+            nc.sync.dma_start(out[nb * P : (nb + 1) * P, :], pages[nb][:])

@@ -18,8 +18,16 @@ P = 128
 HALF = 512
 PAGE_BYTES = 4 * T
 WOVEN_BYTES = 2 * 4 * P
-EARLY = 3 * P
-LATE_AT = 2 * PAGE_BYTES + WOVEN_BYTES
+LAP = 64
+AT_WOVEN0 = 0
+AT_PAGE2 = AT_WOVEN0 + WOVEN_BYTES - LAP
+AT_WOVEN1 = AT_PAGE2 + PAGE_BYTES
+AT_CODES0 = AT_WOVEN1
+AT_PAGE3 = AT_WOVEN1 + WOVEN_BYTES - LAP
+AT_WOVEN23 = AT_PAGE3 + PAGE_BYTES
+AT_CODES23 = AT_WOVEN23 + 2 * WOVEN_BYTES
+AT_RAW23 = AT_CODES23 + 8 * P
+AT_WOVEN_LATE = AT_RAW23 + 4 * WOVEN_BYTES
 
 
 def tile_list_embg_res_none_kernel(tc, dy, w4_words, w4_scales, w8_words, w8_scales, wgo, offs, out):
@@ -38,37 +46,43 @@ def tile_list_embg_res_none_kernel(tc, dy, w4_words, w4_scales, w8_words, w8_sca
         w8 = keep.tile([P, N], U32, name="w8", align_bytes=64)
         s4 = keep.tile([P, N], U8, name="s4", align_bytes=64)
         s8 = keep.tile([P, N], U8, name="s8", align_bytes=64)
-        gain_col = keep.tile([P, 3], F32, name="gain_col")
-        gain = keep.tile([P, J - EARLY], F32, name="gain")
+        gain0 = keep.tile([P, 1], F32, name="gain0")
+        gain123 = keep.tile([P, 3], F32, name="gain123")
+        gain = keep.tile([P, HALF], F32, name="gain")
         ident = keep.tile([P, P], F32, name="ident")
         zeros = keep.tile([P, P], F32, name="zeros")
-        raw = [keep.tile([P, 4, P], F32, name=f"raw{b}", tag=f"raw{b}") for b in range(4)]
-        raw_late = chain.tile([P, 4, HALF], F32, name="raw_late", align_bytes=64, offset=LATE_AT)
+        raw0 = keep.tile([P, 4, P], F32, name="raw0")
+        raw1 = keep.tile([P, 4, P], F32, name="raw1")
+        raw2 = keep.tile([P, 4, P], F32, name="raw2")
+        raw3 = chain.tile([P, 4, P], F32, name="raw3", align_bytes=64, offset=AT_RAW23)
+        raw_late = keep.tile([P, 4, HALF], F32, name="raw_late")
         pages = [keep.tile([P, T], F32, name=f"page{w}") for w in range(2)]
 
-        def load_scales(plane, rows, q):
-            quad = rows[0, 4 * q : 4 * q + 4, :].bitcast(I32)
-            nc.sync.dma_start(plane[32 * q : 32 * q + 32, :].bitcast(I32), quad.partition_broadcast(8))
+        def load_scales(plane, rows):
+            for q in range(4):
+                quad = rows[0, 4 * q : 4 * q + 4, :].bitcast(I32)
+                nc.sync.dma_start(plane[32 * q : 32 * q + 32, :].bitcast(I32), quad.partition_broadcast(8))
 
         def weave(copy, woven, source):
-            copy(out=woven[:].rearrange("p (c i) t -> p c t i", i=2), in_=source[:].rearrange("p t (c i) -> p c t i", i=2))
+            copy(out=woven.rearrange("p (c i) t -> p c t i", i=4), in_=source.rearrange("p t (c i) -> p c t i", i=4))
 
-        def quantise(woven, width, name):
-            codes = keep.tile([P, width], U32, name=f"codes_{name}", align_bytes=64)
+        def quantise(woven, width, name, codes=None):
+            if codes is None:
+                codes = keep.tile([P, width], U32, name=f"codes_{name}", align_bytes=64)
             scales = keep.tile([P, width], U8, name=f"scales_{name}", align_bytes=64)
             nc.vector.quantize_mx(out=codes[:].bitcast(E5M2), scales=scales[:], in_=woven[:].rearrange("p c t -> p (c t)"))
             return codes, scales
 
-        def product_by_token(b, codes, scales):
-            acc = psum.tile([P, N], F32, name=f"tok{b}", tag=("acc0", "acc0", "turn0", "acc3")[b])
-            nc.tensor.matmul_mx(out=acc[:], lhsT=codes[:].bitcast(E5M2), lhsT_scale=scales[:],
+        def product_by_token(name, bank, codes, scales):
+            acc = psum.tile([P, N], F32, name=f"tok{name}", tag=bank)
+            nc.tensor.matmul_mx(out=acc[:], lhsT=codes.bitcast(E5M2), lhsT_scale=scales,
                                 rhs=w4[:].bitcast(E2M1), rhs_scale=s4[:], start=True, stop=False)
-            nc.tensor.matmul_mx(out=acc[:], lhsT=codes[:].bitcast(E5M2), lhsT_scale=scales[:],
+            nc.tensor.matmul_mx(out=acc[:], lhsT=codes.bitcast(E5M2), lhsT_scale=scales,
                                 rhs=w8[:].bitcast(E4M3), rhs_scale=s8[:], start=False, stop=True)
             return acc
 
-        def product_by_row(nb, codes, scales):
-            acc = psum.tile([P, HALF], F32, name=f"row{nb}", tag=f"acc{nb}")
+        def product_by_row(nb, bank, codes, scales):
+            acc = psum.tile([P, HALF], F32, name=f"row{nb}", tag=bank)
             cols = slice(nb * P, (nb + 1) * P)
             nc.tensor.matmul_mx(out=acc[:], lhsT=w4[:, 2 * nb * P : 2 * (nb + 1) * P].bitcast(E2M1), lhsT_scale=s4[:, cols],
                                 rhs=codes[:].bitcast(E5M2), rhs_scale=scales[:], start=True, stop=False)
@@ -76,105 +90,113 @@ def tile_list_embg_res_none_kernel(tc, dy, w4_words, w4_scales, w8_words, w8_sca
                                 rhs=codes[:].bitcast(E5M2), rhs_scale=scales[:], start=False, stop=True)
             return acc
 
-        def turn(sources, name, bank):
-            turned = psum.tile([P, len(sources), P], F32, name=f"turned_{name}", tag=bank)
-            for i, source in enumerate(sources):
-                nc.tensor.transpose(turned[:, i, :], source, ident[:])
+        def turn(by_token, name, bank):
+            count = by_token.shape[1] // P
+            turned = psum.tile([P, count, P], F32, name=f"turned_{name}", tag=bank)
+            for i in range(count):
+                nc.tensor.transpose(turned[:, i, :], by_token[:, i * P : (i + 1) * P], ident[:])
             return turned
 
-        def empty(bank, name, tag=None):
-            dx = keep.tile(list(bank.shape), F32, name=f"dx_{name}", tag=tag or f"dx_{name}")
-            nc.scalar.copy(out=dx[:], in_=bank)
-            return dx
+        def window(nb, a, b):
+            return pages[nb][:].indirect(offsets[:, a // 16 : b // 16])
 
-        def scatter(nb, dx, a, b):
-            window = pages[nb][:].indirect(offsets[:, a // 16 : b // 16])
-            if a < EARLY:
-                nc.vector.tensor_tensor(out=window, in0=dx, in1=zeros[:], op=add)
-            else:
-                nc.vector.tensor_tensor(out=window, in0=dx, in1=gain[:, a - EARLY : b - EARLY], op=mult)
+        def scatter_block(nb, dx, a):
+            nc.vector.tensor_tensor(out=window(nb, a, a + P), in0=dx, in1=zeros[:], op=add)
 
-        for q in range(3):
-            load_scales(s4, w4_scales, q)
-        nc.sync.dma_start(raw[0][:], dy_rows[:, :, :P])
-        load_scales(s4, w4_scales, 3)
-        for q in range(3):
-            load_scales(s8, w8_scales, q)
+        def load_gain_columns(column, first, count):
+            with nc.allow_non_contiguous_dma(reason="one weight a partition"):
+                nc.sync.dma_start(column[:], wgo[0, first * P : (first + count) * P].rearrange("(b p) -> p b", p=P))
+
+        load_scales(s4, w4_scales)
+        nc.sync.dma_start(raw0[:], dy_rows[:, :, :P])
         nc.sync.dma_start(w4[:].bitcast(I32), w4_words[0].bitcast(I32))
-        load_scales(s8, w8_scales, 3)
         nc.sync.dma_start(w8[:].bitcast(I32), w8_words[0].rearrange("p n t -> p (n t)").bitcast(I32))
-        with nc.allow_non_contiguous_dma(reason="one weight a partition"):
-            nc.sync.dma_start(gain_col[:], wgo[0, :EARLY].rearrange("(b p) -> p b", p=P))
-        nc.sync.dma_start(raw[1][:], dy_rows[:, :, P : 2 * P])
+        load_scales(s8, w8_scales)
+        nc.sync.dma_start(raw1[:], dy_rows[:, :, P : 2 * P])
+        load_gain_columns(gain0, 0, 1)
+        nc.sync.dma_start(raw2[:], dy_rows[:, :, 2 * P : 3 * P])
         nc.sync.dma_start(offsets[:], offs)
-        for b in (2, 3):
-            nc.sync.dma_start(raw[b][:], dy_rows[:, :, b * P : (b + 1) * P])
+        nc.sync.dma_start(raw3[:], dy_rows[:, :, 3 * P : HALF])
+        load_gain_columns(gain123, 1, 3)
         nc.sync.dma_start(raw_late[:], dy_rows[:, :, HALF:])
-        nc.sync.dma_start(gain[:], wgo[:, EARLY:])
+        nc.sync.dma_start(gain[:], wgo[:, HALF:])
 
         make_identity(nc, ident[:])
         nc.scalar.activation(out=zeros[:], in_=ident[:], func=copy_fn, scale=0.0)
         for page in pages:
             nc.vector.memset(page[:].bitcast(I32), 0)
 
-        step = WOVEN_BYTES // 2
-        woven = chain.tile([P, P, 4], BF16, name="woven0", align_bytes=64, offset=PAGE_BYTES - step)
-        weave(nc.vector.tensor_copy, woven, raw[0])
-        blocks = [quantise(woven, P, "b0")]
-        pages.append(chain.tile([P, T], F32, name="page2", align_bytes=64, offset=0))
+
+        woven0 = chain.tile([P, P, 4], BF16, name="woven0", align_bytes=64, offset=AT_WOVEN0)
+        weave(nc.vector.tensor_copy, woven0[:], raw0[:])
+        codes0 = chain.tile([P, P], U32, name="codes_b0", align_bytes=64, offset=AT_CODES0)
+        codes0, scales0 = quantise(woven0, P, "b0", codes0)
+        pages.append(chain.tile([P, T], F32, name="page2", align_bytes=64, offset=AT_PAGE2))
         nc.vector.memset(pages[2][:].bitcast(I32), 0)
-        for b in (1, 2):
-            woven = chain.tile([P, P, 4], BF16, name=f"woven{b}", align_bytes=64, offset=PAGE_BYTES + (b - 1) * step)
-            weave(nc.vector.tensor_copy, woven, raw[b])
-            blocks.append(quantise(woven, P, f"b{b}"))
-        pages.append(chain.tile([P, T], F32, name="page3", align_bytes=64, offset=PAGE_BYTES + 2 * step))
+
+        acc = product_by_token("0", "acc", codes0[:], scales0[:])
+        woven1 = chain.tile([P, P, 4], BF16, name="woven1", align_bytes=64, offset=AT_WOVEN1)
+        weave(nc.vector.tensor_copy, woven1[:], raw1[:])
+        codes1, scales1 = quantise(woven1, P, "b1")
+        pages.append(chain.tile([P, T], F32, name="page3", align_bytes=64, offset=AT_PAGE3))
         nc.gpsimd.memset(pages[3][:], 0.0)
-
-        acc = product_by_token(0, *blocks[0])
-        by_token = keep.tile([P, N], F32, name="by_token0", tag="by_token0", align_bytes=64)
-        nc.scalar.activation(out=by_token[:, :P], in_=acc[:, :P], func=copy_fn, scale=gain_col[:, 0:1])
-        head = turn([by_token[:, :P]], "head", "turn0")
-        nc.scalar.activation(out=by_token[:, P:], in_=acc[:, P:], func=copy_fn, scale=gain_col[:, 0:1])
-        scatter(0, empty(head[:], "head")[:, 0, :], 0, P)
-        rest = turn([by_token[:, nb * P : (nb + 1) * P] for nb in (1, 2, 3)], "rest", "turn1")
-        dx = empty(rest[:], "rest")
-        for nb in (1, 2, 3):
-            scatter(nb, dx[:, nb - 1, :], 0, P)
-
-        def turned_block(b, bank):
-            acc = product_by_token(b, *blocks[b])
-            if b * P < EARLY:
-                by_token = keep.tile([P, N], F32, name=f"by_token{b}", tag=f"by_token{b}", align_bytes=64)
-                nc.scalar.activation(out=by_token[:], in_=acc[:], func=copy_fn, scale=gain_col[:, b : b + 1])
-            else:
-                by_token = chain.tile([P, N], F32, name=f"by_token{b}", align_bytes=64, offset=LATE_AT + 4 * N)
-                nc.scalar.copy(out=by_token[:], in_=acc[:])
-            return turn([by_token[:, nb * P : (nb + 1) * P] for nb in range(4)], f"b{b}", bank)
-
-        turned1 = turned_block(1, "turn2")
-        dx = empty(turned1[:, :2, :], "b1_low")
-        for nb in (0, 1):
-            scatter(nb, dx[:, nb, :], P, 2 * P)
-        turned2 = turned_block(2, "turn0")
-        woven = keep.tile([P, P, 4], BF16, name="woven3", tag="by_token1", align_bytes=64)
-        weave(nc.scalar.copy, woven, raw[3])
-        blocks.append(quantise(woven, P, "b3"))
-        dx = empty(turned1[:, 2:, :], "b1_high", "raw3")
+        first = chain.tile([P, P], F32, name="first", align_bytes=64, offset=AT_WOVEN23)
+        nc.scalar.activation(out=first[:], in_=acc[:, :P], func=copy_fn, scale=gain0[:])
+        turned_a = turn(first[:], "0a", "turn0")
+        rest = keep.tile([P, 3 * P], F32, name="rest")
+        nc.scalar.activation(out=rest[:], in_=acc[:, P:], func=copy_fn, scale=gain0[:])
+        dx_a = chain.tile([P, P], F32, name="dx_a", align_bytes=64, offset=AT_CODES23)
+        nc.vector.tensor_copy(out=dx_a[:], in_=turned_a[:, 0, :])
+        scatter_block(0, dx_a[:], 0)
+        woven23 = chain.tile([P, 2 * P, 4], BF16, name="woven23", align_bytes=64, offset=AT_WOVEN23)
+        weave(nc.scalar.copy, woven23[:, :P, :], raw2[:])
+        turned_b = turn(rest[:, :P], "0b", "turn2")
+        turned_cd = turn(rest[:, P:], "0cd", "turn1")
+        dx_b = keep.tile([P, P], F32, name="dx_b")
+        nc.scalar.copy(out=dx_b[:], in_=turned_b[:, 0, :])
+        scatter_block(1, dx_b[:], 0)
+        weave(nc.scalar.copy, woven23[:, P:, :], raw3[:])
+        codes23 = chain.tile([P, 2 * P], U32, name="codes_b23", align_bytes=64, offset=AT_CODES23)
+        codes23, scales23 = quantise(woven23, 2 * P, "b23", codes23)
+        dx_cd = chain.tile([P, 2, P], F32, name="dx_cd", align_bytes=64, offset=AT_RAW23)
+        nc.scalar.copy(out=dx_cd[:], in_=turned_cd[:])
         for nb in (2, 3):
-            scatter(nb, dx[:, nb - 2, :], P, 2 * P)
+            scatter_block(nb, dx_cd[:, nb - 2, :], 0)
 
-        woven = keep.tile([P, HALF, 4], BF16, name="woven_late", tag="by_token2", align_bytes=64)
-        weave(nc.scalar.copy, woven, raw_late)
-        late = quantise(woven, HALF, "late")
-        dx = chain.tile([P, 4, P], F32, name="dx_b2", align_bytes=64, offset=LATE_AT)
-        nc.scalar.copy(out=dx[:], in_=turned2[:])
+        acc = product_by_token("1", "acc", codes1[:], scales1[:])
+        by_token1 = keep.tile([P, N], F32, name="by_token1")
+        dx1 = keep.tile([P, 4, P], F32, name="dx1")
+        halves = []
+        for h in range(2):
+            cols = slice(2 * h * P, 2 * (h + 1) * P)
+            nc.scalar.activation(out=by_token1[:, cols], in_=acc[:, cols], func=copy_fn, scale=gain123[:, 0:1])
+            halves.append(turn(by_token1[:, cols], f"1{h}", ("turn0", "turn2")[h]))
+        for h in range(2):
+            nc.scalar.copy(out=dx1[:, 2 * h : 2 * h + 2, :], in_=halves[h][:])
+            for nb in (2 * h, 2 * h + 1):
+                scatter_block(nb, dx1[:, nb, :], P)
+        by_token23 = [keep.tile([P, N], F32, name="by_token2"),
+                      chain.tile([P, N], F32, name="by_token3", align_bytes=64, offset=AT_WOVEN_LATE)]
+        for i, by_token in enumerate(by_token23):
+            cols = slice(i * P, (i + 1) * P)
+            acc = product_by_token(str(2 + i), ("acc", "acc3")[i], codes23[:, cols], scales23[:, cols])
+            nc.scalar.activation(out=by_token[:], in_=acc[:], func=copy_fn, scale=gain123[:, 1 + i : 2 + i])
+        turned2 = turn(by_token23[0][:], "2", "turn1")
+        turned3 = turn(by_token23[1][:], "3", "turn0")
+        dx2 = keep.tile([P, 4, P], F32, name="dx2")
+        nc.scalar.copy(out=dx2[:], in_=turned2[:])
         for nb in range(4):
-            scatter(nb, dx[:, nb, :], 2 * P, EARLY)
+            scatter_block(nb, dx2[:, nb, :], 2 * P)
+        woven_late = chain.tile([P, HALF, 4], BF16, name="woven_late", align_bytes=64, offset=AT_WOVEN_LATE)
+        weave(nc.scalar.copy, woven_late[:], raw_late[:])
+        late = quantise(woven_late, HALF, "late")
+        dx3 = keep.tile([P, 4, P], F32, name="dx3")
+        nc.scalar.copy(out=dx3[:], in_=turned3[:])
+        for nb in range(4):
+            scatter_block(nb, dx3[:, nb, :], 3 * P)
 
-        turned3 = turned_block(3, "turn1")
         for nb in range(4):
-            tail = keep.tile([P, J - EARLY], F32, name=f"tail{nb}")
-            nc.scalar.copy(out=tail[:, :P], in_=turned3[:, nb, :])
-            nc.scalar.copy(out=tail[:, P:], in_=product_by_row(nb, *late)[:])
-            scatter(nb, tail[:], EARLY, J)
+            tail = keep.tile([P, HALF], F32, name=f"tail{nb}")
+            nc.scalar.copy(out=tail[:], in_=product_by_row(nb, ("late0", "late1", "late2", "acc3")[nb], *late)[:])
+            nc.vector.tensor_tensor(out=window(nb, HALF, J), in0=tail[:], in1=gain[:], op=mult)
             nc.sync.dma_start(out[nb * P : (nb + 1) * P, :], pages[nb][:])

@@ -19,15 +19,16 @@ HALF = 512
 PAGE_BYTES = 4 * T
 WOVEN_BYTES = 2 * 4 * P
 LAP = 64
-AT_WOVEN0 = 0
+VECTOR_SHARE = 80
+AT_PAGE3 = 0
+AT_WOVEN1 = AT_PAGE3 + PAGE_BYTES - LAP
+AT_WOVEN0 = AT_WOVEN1 + WOVEN_BYTES - LAP
 AT_PAGE2 = AT_WOVEN0 + WOVEN_BYTES - LAP
-AT_WOVEN1 = AT_PAGE2 + PAGE_BYTES
-AT_CODES0 = AT_WOVEN1
-AT_PAGE3 = AT_WOVEN1 + WOVEN_BYTES - LAP
-AT_WOVEN23 = AT_PAGE3 + PAGE_BYTES
-AT_CODES23 = AT_WOVEN23 + 2 * WOVEN_BYTES
-AT_RAW23 = AT_CODES23 + 8 * P
-AT_WOVEN_LATE = AT_RAW23 + 4 * WOVEN_BYTES
+AT_REST = AT_PAGE2 + PAGE_BYTES
+AT_BY_TOKEN1 = AT_REST + 4 * 3 * P
+AT_RAW23 = AT_BY_TOKEN1 + 4 * N
+AT_RAW_LATE = AT_RAW23 + 4 * 4 * 2 * P
+AT_BY_TOKEN2 = AT_RAW_LATE + 4 * 4 * HALF
 
 
 def tile_list_embg_res_none_kernel(tc, dy, w4_words, w4_scales, w8_words, w8_scales, wgo, offs, out):
@@ -46,22 +47,22 @@ def tile_list_embg_res_none_kernel(tc, dy, w4_words, w4_scales, w8_words, w8_sca
         w8 = keep.tile([P, N], U32, name="w8", align_bytes=64)
         s4 = keep.tile([P, N], U8, name="s4", align_bytes=64)
         s8 = keep.tile([P, N], U8, name="s8", align_bytes=64)
-        gain0 = keep.tile([P, 1], F32, name="gain0")
-        gain123 = keep.tile([P, 3], F32, name="gain123")
+        columns = [keep.tile([P, 8], F32, name=f"column{b}") for b in range(4)]
         gain = keep.tile([P, HALF], F32, name="gain")
         ident = keep.tile([P, P], F32, name="ident")
         zeros = keep.tile([P, P], F32, name="zeros")
         raw0 = keep.tile([P, 4, P], F32, name="raw0")
         raw1 = keep.tile([P, 4, P], F32, name="raw1")
-        raw2 = keep.tile([P, 4, P], F32, name="raw2")
-        raw3 = chain.tile([P, 4, P], F32, name="raw3", align_bytes=64, offset=AT_RAW23)
-        raw_late = keep.tile([P, 4, HALF], F32, name="raw_late")
+        raw23 = chain.tile([P, 4, 2 * P], F32, name="raw23", align_bytes=64, offset=AT_RAW23)
+        raw_late = chain.tile([P, 4, HALF], F32, name="raw_late", align_bytes=64, offset=AT_RAW_LATE)
         pages = [keep.tile([P, T], F32, name=f"page{w}") for w in range(2)]
 
-        def load_scales(plane, rows):
-            for q in range(4):
-                quad = rows[0, 4 * q : 4 * q + 4, :].bitcast(I32)
-                nc.sync.dma_start(plane[32 * q : 32 * q + 32, :].bitcast(I32), quad.partition_broadcast(8))
+        def load_scale_rows(queue, plane, rows, q):
+            quad = rows[0, 4 * q : 4 * q + 4, :].bitcast(I32)
+            if plane is s4:
+                queue.dma_start(plane[32 * q : 32 * q + 32, :].bitcast(I32), quad.partition_broadcast(8))
+            else:
+                queue.dma_start(plane[32 * q : 32 * q + 4, :].bitcast(I32), quad)
 
         def weave(copy, woven, source):
             copy(out=woven.rearrange("p (c i) t -> p c t i", i=4), in_=source.rearrange("p t (c i) -> p c t i", i=4))
@@ -103,22 +104,30 @@ def tile_list_embg_res_none_kernel(tc, dy, w4_words, w4_scales, w8_words, w8_sca
         def scatter_block(nb, dx, a):
             nc.vector.tensor_tensor(out=window(nb, a, a + P), in0=dx, in1=zeros[:], op=add)
 
-        def load_gain_columns(column, first, count):
-            with nc.allow_non_contiguous_dma(reason="one weight a partition"):
-                nc.sync.dma_start(column[:], wgo[0, first * P : (first + count) * P].rearrange("(b p) -> p b", p=P))
+        def load_gain_column(queue, block):
+            rows = wgo.rearrange("r j -> (r j)")[: 8 * (J + 1)].rearrange("(v x) -> v x", v=8)
+            queue.dma_start(columns[block][:], rows[:, block * P : (block + 1) * P].rearrange("v (u c) -> u v c", c=8))
 
-        load_scales(s4, w4_scales)
+        nc.gpsimd.memset(s8[:].bitcast(I32), 0)
+        load_scale_rows(nc.sync, s4, w4_scales, 0)
+        load_scale_rows(nc.sync, s4, w4_scales, 1)
+        load_scale_rows(nc.sync, s4, w4_scales, 2)
         nc.sync.dma_start(raw0[:], dy_rows[:, :, :P])
+        load_scale_rows(nc.sync, s4, w4_scales, 3)
         nc.sync.dma_start(w4[:].bitcast(I32), w4_words[0].bitcast(I32))
         nc.sync.dma_start(w8[:].bitcast(I32), w8_words[0].rearrange("p n t -> p (n t)").bitcast(I32))
-        load_scales(s8, w8_scales)
+        load_scale_rows(nc.sync, s8, w8_scales, 0)
+        load_scale_rows(nc.sync, s8, w8_scales, 1)
+        load_scale_rows(nc.sync, s8, w8_scales, 2)
+        load_scale_rows(nc.sync, s8, w8_scales, 3)
+        load_gain_column(nc.sync, 0)
         nc.sync.dma_start(raw1[:], dy_rows[:, :, P : 2 * P])
-        load_gain_columns(gain0, 0, 1)
-        nc.sync.dma_start(raw2[:], dy_rows[:, :, 2 * P : 3 * P])
         nc.sync.dma_start(offsets[:], offs)
-        nc.sync.dma_start(raw3[:], dy_rows[:, :, 3 * P : HALF])
-        load_gain_columns(gain123, 1, 3)
+        nc.sync.dma_start(raw23[:], dy_rows[:, :, 2 * P : HALF])
+        load_gain_column(nc.sync, 1)
         nc.sync.dma_start(raw_late[:], dy_rows[:, :, HALF:])
+        load_gain_column(nc.sync, 2)
+        load_gain_column(nc.sync, 3)
         nc.sync.dma_start(gain[:], wgo[:, HALF:])
 
         make_identity(nc, ident[:])
@@ -128,9 +137,9 @@ def tile_list_embg_res_none_kernel(tc, dy, w4_words, w4_scales, w8_words, w8_sca
 
 
         woven0 = chain.tile([P, P, 4], BF16, name="woven0", align_bytes=64, offset=AT_WOVEN0)
-        weave(nc.vector.tensor_copy, woven0[:], raw0[:])
-        codes0 = chain.tile([P, P], U32, name="codes_b0", align_bytes=64, offset=AT_CODES0)
-        codes0, scales0 = quantise(woven0, P, "b0", codes0)
+        weave(nc.vector.tensor_copy, woven0[:, :VECTOR_SHARE, :], raw0[:, :, :VECTOR_SHARE])
+        weave(nc.scalar.copy, woven0[:, VECTOR_SHARE:, :], raw0[:, :, VECTOR_SHARE:])
+        codes0, scales0 = quantise(woven0, P, "b0")
         pages.append(chain.tile([P, T], F32, name="page2", align_bytes=64, offset=AT_PAGE2))
         nc.vector.memset(pages[2][:].bitcast(I32), 0)
 
@@ -140,63 +149,85 @@ def tile_list_embg_res_none_kernel(tc, dy, w4_words, w4_scales, w8_words, w8_sca
         codes1, scales1 = quantise(woven1, P, "b1")
         pages.append(chain.tile([P, T], F32, name="page3", align_bytes=64, offset=AT_PAGE3))
         nc.gpsimd.memset(pages[3][:], 0.0)
-        first = chain.tile([P, P], F32, name="first", align_bytes=64, offset=AT_WOVEN23)
-        nc.scalar.activation(out=first[:], in_=acc[:, :P], func=copy_fn, scale=gain0[:])
+        first = keep.tile([P, P], F32, name="first")
+        nc.scalar.activation(out=first[:], in_=acc[:, :P], func=copy_fn, scale=columns[0][:, 0:1])
         turned_a = turn(first[:], "0a", "turn0")
-        rest = keep.tile([P, 3 * P], F32, name="rest")
-        nc.scalar.activation(out=rest[:], in_=acc[:, P:], func=copy_fn, scale=gain0[:])
-        dx_a = chain.tile([P, P], F32, name="dx_a", align_bytes=64, offset=AT_CODES23)
+        rest = chain.tile([P, 3 * P], F32, name="rest", align_bytes=64, offset=AT_REST)
+        nc.scalar.activation(out=rest[:], in_=acc[:, P:], func=copy_fn, scale=columns[0][:, 0:1])
+        dx_a = keep.tile([P, P], F32, name="dx_a")
         nc.vector.tensor_copy(out=dx_a[:], in_=turned_a[:, 0, :])
         scatter_block(0, dx_a[:], 0)
-        woven23 = chain.tile([P, 2 * P, 4], BF16, name="woven23", align_bytes=64, offset=AT_WOVEN23)
-        weave(nc.scalar.copy, woven23[:, :P, :], raw2[:])
         turned_b = turn(rest[:, :P], "0b", "turn2")
         turned_cd = turn(rest[:, P:], "0cd", "turn1")
         dx_b = keep.tile([P, P], F32, name="dx_b")
         nc.scalar.copy(out=dx_b[:], in_=turned_b[:, 0, :])
         scatter_block(1, dx_b[:], 0)
-        weave(nc.scalar.copy, woven23[:, P:, :], raw3[:])
-        codes23 = chain.tile([P, 2 * P], U32, name="codes_b23", align_bytes=64, offset=AT_CODES23)
-        codes23, scales23 = quantise(woven23, 2 * P, "b23", codes23)
-        dx_cd = chain.tile([P, 2, P], F32, name="dx_cd", align_bytes=64, offset=AT_RAW23)
-        nc.scalar.copy(out=dx_cd[:], in_=turned_cd[:])
-        for nb in (2, 3):
-            scatter_block(nb, dx_cd[:, nb - 2, :], 0)
+        dx_c = keep.tile([P, P], F32, name="dx_c")
+        nc.scalar.copy(out=dx_c[:], in_=turned_cd[:, 0, :])
+        scatter_block(2, dx_c[:], 0)
+        woven2 = chain.tile([P, P, 4], BF16, name="woven2", align_bytes=64, offset=AT_REST)
+        weave(nc.scalar.copy, woven2[:], raw23[:, :, :P])
+        codes2, scales2 = quantise(woven2, P, "b2")
+        dx_d = keep.tile([P, P], F32, name="dx_d")
+        nc.scalar.copy(out=dx_d[:], in_=turned_cd[:, 1, :])
+        scatter_block(3, dx_d[:], 0)
 
         acc = product_by_token("1", "acc", codes1[:], scales1[:])
-        by_token1 = keep.tile([P, N], F32, name="by_token1")
-        dx1 = keep.tile([P, 4, P], F32, name="dx1")
+        by_token1 = chain.tile([P, N], F32, name="by_token1", align_bytes=64, offset=AT_BY_TOKEN1)
+        dx1_ab = keep.tile([P, 2, P], F32, name="dx1_ab")
+        nc.scalar.activation(out=by_token1[:, :P], in_=acc[:, :P], func=copy_fn, scale=columns[1][:, 0:1])
+        turned_a = turn(by_token1[:, :P], "1a", "turn0")
+        nc.scalar.activation(out=by_token1[:, P:], in_=acc[:, P:], func=copy_fn, scale=columns[1][:, 0:1])
+        turned_b = turn(by_token1[:, P : 2 * P], "1b", "turn2")
+        turned_cd = turn(by_token1[:, 2 * P :], "1cd", "turn1")
+        for nb, turned in enumerate((turned_a, turned_b)):
+            nc.scalar.copy(out=dx1_ab[:, nb, :], in_=turned[:, 0, :])
+            scatter_block(nb, dx1_ab[:, nb, :], P)
+        woven3 = chain.tile([P, P, 4], BF16, name="woven3", align_bytes=64, offset=AT_BY_TOKEN1)
+        weave(nc.scalar.copy, woven3[:], raw23[:, :, P:])
+        codes3, scales3 = quantise(woven3, P, "b3")
+        dx1_cd = chain.tile([P, 2, P], F32, name="dx1_cd", align_bytes=64, offset=AT_RAW23 + 2 * WOVEN_BYTES)
+        nc.scalar.copy(out=dx1_cd[:], in_=turned_cd[:])
+        for nb in (2, 3):
+            scatter_block(nb, dx1_cd[:, nb - 2, :], P)
+
+        acc = product_by_token("2", "acc", codes2[:], scales2[:])
+        by_token2 = chain.tile([P, N], F32, name="by_token2", align_bytes=64, offset=AT_BY_TOKEN2)
         halves = []
         for h in range(2):
             cols = slice(2 * h * P, 2 * (h + 1) * P)
-            nc.scalar.activation(out=by_token1[:, cols], in_=acc[:, cols], func=copy_fn, scale=gain123[:, 0:1])
-            halves.append(turn(by_token1[:, cols], f"1{h}", ("turn0", "turn2")[h]))
-        for h in range(2):
-            nc.scalar.copy(out=dx1[:, 2 * h : 2 * h + 2, :], in_=halves[h][:])
-            for nb in (2 * h, 2 * h + 1):
-                scatter_block(nb, dx1[:, nb, :], P)
-        by_token23 = [keep.tile([P, N], F32, name="by_token2"),
-                      chain.tile([P, N], F32, name="by_token3", align_bytes=64, offset=AT_WOVEN_LATE)]
-        for i, by_token in enumerate(by_token23):
-            cols = slice(i * P, (i + 1) * P)
-            acc = product_by_token(str(2 + i), ("acc", "acc3")[i], codes23[:, cols], scales23[:, cols])
-            nc.scalar.activation(out=by_token[:], in_=acc[:], func=copy_fn, scale=gain123[:, 1 + i : 2 + i])
-        turned2 = turn(by_token23[0][:], "2", "turn1")
-        turned3 = turn(by_token23[1][:], "3", "turn0")
+            nc.scalar.activation(out=by_token2[:, cols], in_=acc[:, cols], func=copy_fn, scale=columns[2][:, 0:1])
+            halves.append(turn(by_token2[:, cols], f"2{h}", ("turn0", "turn1")[h]))
         dx2 = keep.tile([P, 4, P], F32, name="dx2")
-        nc.scalar.copy(out=dx2[:], in_=turned2[:])
-        for nb in range(4):
-            scatter_block(nb, dx2[:, nb, :], 2 * P)
-        woven_late = chain.tile([P, HALF, 4], BF16, name="woven_late", align_bytes=64, offset=AT_WOVEN_LATE)
-        weave(nc.scalar.copy, woven_late[:], raw_late[:])
-        late = quantise(woven_late, HALF, "late")
+        for h in range(2):
+            nc.scalar.copy(out=dx2[:, 2 * h : 2 * h + 2, :], in_=halves[h][:])
+            for nb in (2 * h, 2 * h + 1):
+                scatter_block(nb, dx2[:, nb, :], 2 * P)
+        late = (keep.tile([P, HALF], U32, name="codes_late", align_bytes=64),
+                keep.tile([P, HALF], U8, name="scales_late", align_bytes=64))
+        for part, at in enumerate((AT_RAW23, AT_BY_TOKEN2)):
+            woven = chain.tile([P, 2 * P, 4], BF16, name=f"woven_late{part}", align_bytes=64, offset=at)
+            for piece in range(2):
+                first_col = (2 * part + piece) * P
+                weave(nc.scalar.copy, woven[:, piece * P : (piece + 1) * P, :], raw_late[:, :, first_col : first_col + P])
+            cols = slice(2 * part * P, 2 * (part + 1) * P)
+            nc.vector.quantize_mx(out=late[0][:, cols].bitcast(E5M2), scales=late[1][:, cols],
+                                  in_=woven[:].rearrange("p c t -> p (c t)"))
+        acc = product_by_token("3", "acc", codes3[:], scales3[:])
+        by_token3 = chain.tile([P, N], F32, name="by_token3", align_bytes=64, offset=AT_RAW_LATE)
+        halves = []
+        for h in range(2):
+            cols = slice(2 * h * P, 2 * (h + 1) * P)
+            nc.scalar.activation(out=by_token3[:, cols], in_=acc[:, cols], func=copy_fn, scale=columns[3][:, 0:1])
+            halves.append(turn(by_token3[:, cols], f"3{h}", ("turn2", "turn0")[h]))
         dx3 = keep.tile([P, 4, P], F32, name="dx3")
-        nc.scalar.copy(out=dx3[:], in_=turned3[:])
-        for nb in range(4):
-            scatter_block(nb, dx3[:, nb, :], 3 * P)
+        for h in range(2):
+            nc.scalar.copy(out=dx3[:, 2 * h : 2 * h + 2, :], in_=halves[h][:])
+            for nb in (2 * h, 2 * h + 1):
+                scatter_block(nb, dx3[:, nb, :], 3 * P)
 
         for nb in range(4):
             tail = keep.tile([P, HALF], F32, name=f"tail{nb}")
-            nc.scalar.copy(out=tail[:], in_=product_by_row(nb, ("late0", "late1", "late2", "acc3")[nb], *late)[:])
+            nc.scalar.copy(out=tail[:], in_=product_by_row(nb, "turn0", *late)[:])
             nc.vector.tensor_tensor(out=window(nb, HALF, J), in0=tail[:], in1=gain[:], op=mult)
             nc.sync.dma_start(out[nb * P : (nb + 1) * P, :], pages[nb][:])

@@ -47,7 +47,7 @@ def tile_list_embg_res_none_kernel(tc, dy, w4_words, w4_scales, w8_words, w8_sca
         w8 = keep.tile([P, N], U32, name="w8", align_bytes=64)
         s4 = keep.tile([P, N], U8, name="s4", align_bytes=64)
         s8 = keep.tile([P, N], U8, name="s8", align_bytes=64)
-        columns = [keep.tile([P, 8], F32, name=f"column{b}") for b in range(4)]
+        columns = [keep.tile([P, 1], F32, name=f"column{b}") for b in range(4)]
         gain = keep.tile([P, HALF], F32, name="gain")
         ident = keep.tile([P, P], F32, name="ident")
         zeros = keep.tile([P, P], F32, name="zeros")
@@ -105,8 +105,8 @@ def tile_list_embg_res_none_kernel(tc, dy, w4_words, w4_scales, w8_words, w8_sca
             nc.vector.tensor_tensor(out=window(nb, a, a + P), in0=dx, in1=zeros[:], op=add)
 
         def load_gain_column(queue, block):
-            rows = wgo.rearrange("r j -> (r j)")[: 8 * (J + 1)].rearrange("(v x) -> v x", v=8)
-            queue.dma_start(columns[block][:], rows[:, block * P : (block + 1) * P].rearrange("v (u c) -> u v c", c=8))
+            with nc.allow_non_contiguous_dma(reason="one weight a partition"):
+                queue.dma_start(columns[block][:], wgo[0, block * P : (block + 1) * P].rearrange("(b p) -> p b", p=P))
 
         nc.gpsimd.memset(s8[:].bitcast(I32), 0)
         load_scale_rows(nc.sync, s4, w4_scales, 0)

@@ -1,5 +1,4 @@
 import concourse.mybir as mybir
-from concourse.masks import make_identity
 
 K, N, T, J = 512, 512, 2048, 1024
 FLOPS = 2 * 2 * K * N * J
@@ -15,219 +14,169 @@ E4M3 = mybir.dt.float8_e4m3fn_x4
 E2M1 = mybir.dt.float4_e2m1fn_x4
 
 P = 128
-HALF = 512
-PAGE_BYTES = 4 * T
-WOVEN_BYTES = 2 * 4 * P
-LAP = 64
+BANK = 512
+REPEATED_ROWS = 14
 VECTOR_SHARE = 80
-AT_PAGE3 = 0
-AT_WOVEN1 = AT_PAGE3 + PAGE_BYTES - LAP
-AT_WOVEN0 = AT_WOVEN1 + WOVEN_BYTES - LAP
-AT_PAGE2 = AT_WOVEN0 + WOVEN_BYTES - LAP
-AT_REST = AT_PAGE2 + PAGE_BYTES
-AT_BY_TOKEN1 = AT_REST + 4 * 3 * P
-AT_RAW23 = AT_BY_TOKEN1 + 4 * N
-AT_RAW_LATE = AT_RAW23 + 4 * 4 * 2 * P
-AT_BY_TOKEN2 = AT_RAW_LATE + 4 * 4 * HALF
+PAGE_BYTES = 4 * T
+AT_FIRST_DX = PAGE_BYTES + 16 * J
 
 
 def tile_list_embg_res_none_kernel(tc, dy, w4_words, w4_scales, w8_words, w8_scales, wgo, offs, out):
     nc = tc.nc
     mult, add = mybir.AluOpType.mult, mybir.AluOpType.add
-    copy_fn = mybir.ActivationFunctionType.Copy
     dy_rows = dy.rearrange("(p t) j -> p t j", t=4)
 
     with (
         tc.tile_pool(name="keep", bufs=1) as keep,
-        tc.tile_pool(name="chain", bufs=1) as chain,
+        tc.tile_pool(name="shared", bufs=1) as shared,
         tc.psum_pool(name="psum", bufs=1) as psum,
     ):
         offsets = keep.tile([P, J // 16], U16, name="offsets")
-        w4 = keep.tile([P, 2 * N], U8, name="w4", align_bytes=64)
-        w8 = keep.tile([P, N], U32, name="w8", align_bytes=64)
-        s4 = keep.tile([P, N], U8, name="s4", align_bytes=64)
-        s8 = keep.tile([P, N], U8, name="s8", align_bytes=64)
-        columns = [keep.tile([P, 1], F32, name=f"column{b}") for b in range(4)]
-        gain = keep.tile([P, HALF], F32, name="gain")
-        ident = keep.tile([P, P], F32, name="ident")
+        w4 = [keep.tile([P, N], U8, name=f"w4_{h}", align_bytes=64) for h in range(2)]
+        w8 = [keep.tile([P, N // 2], U32, name=f"w8_{h}", align_bytes=64) for h in range(2)]
+        planes = keep.tile([P, 2 * N], U8, name="planes", align_bytes=64)
+        s4, s8 = planes[:, :N], planes[:, N:]
+        gain = keep.tile([P, J], F32, name="gain")
         zeros = keep.tile([P, P], F32, name="zeros")
-        raw0 = keep.tile([P, 4, P], F32, name="raw0")
-        raw1 = keep.tile([P, 4, P], F32, name="raw1")
-        raw23 = chain.tile([P, 4, 2 * P], F32, name="raw23", align_bytes=64, offset=AT_RAW23)
-        raw_late = chain.tile([P, 4, HALF], F32, name="raw_late", align_bytes=64, offset=AT_RAW_LATE)
+        codes = keep.tile([P, J], U32, name="codes", align_bytes=64)
+        scales = keep.tile([P, J], U8, name="scales", align_bytes=64)
         pages = [keep.tile([P, T], F32, name=f"page{w}") for w in range(2)]
+        spans = ((0, 128), (128, 256), (256, 384), (384, 512), (512, 768), (768, 1024))
+        loads = ((0, 256), (256, 384), (384, 512), (512, 768), (768, 1024))
+        raw = {a: shared.tile([P, 4, b - a], F32, name=f"raw{a}", align_bytes=64, offset=PAGE_BYTES + 16 * a) for a, b in loads}
+        dx = {}
+        woven = {i: keep.tile([P, b - a, 4], BF16, name=f"woven{a}", align_bytes=64) for i, (a, b) in enumerate(spans) if i not in (1, 2)}
+        woven[1] = shared.tile([P, P, 4], BF16, name="woven128", align_bytes=64, offset=0)
 
-        def load_scale_rows(queue, plane, rows, q):
-            quad = rows[0, 4 * q : 4 * q + 4, :].bitcast(I32)
-            if plane is s4:
-                queue.dma_start(plane[32 * q : 32 * q + 32, :].bitcast(I32), quad.partition_broadcast(8))
-            else:
-                queue.dma_start(plane[32 * q : 32 * q + 4, :].bitcast(I32), quad)
+        def load_first_scale_rows(queue, plane, rows):
+            source = rows[0, :REPEATED_ROWS, :].bitcast(I32).partition_broadcast(7)
+            queue.dma_start(plane[: 7 * REPEATED_ROWS, :].bitcast(I32), source)
 
-        def weave(copy, woven, source):
-            copy(out=woven.rearrange("p (c i) t -> p c t i", i=4), in_=source.rearrange("p t (c i) -> p c t i", i=4))
+        def load_last_scale_rows(queue, plane, rows):
+            queue.dma_start(plane[98:100, :].bitcast(I32), rows[0, REPEATED_ROWS:, :].bitcast(I32))
 
-        def quantise(woven, width, name, codes=None):
-            if codes is None:
-                codes = keep.tile([P, width], U32, name=f"codes_{name}", align_bytes=64)
-            scales = keep.tile([P, width], U8, name=f"scales_{name}", align_bytes=64)
-            nc.vector.quantize_mx(out=codes[:].bitcast(E5M2), scales=scales[:], in_=woven[:].rearrange("p c t -> p (c t)"))
-            return codes, scales
+        def load_dy(i):
+            a, b = loads[i]
+            nc.sync.dma_start(raw[a][:], dy_rows[:, :, a:b])
 
-        def product_by_token(name, bank, codes, scales):
-            acc = psum.tile([P, N], F32, name=f"tok{name}", tag=bank)
-            nc.tensor.matmul_mx(out=acc[:], lhsT=codes.bitcast(E5M2), lhsT_scale=scales,
-                                rhs=w4[:].bitcast(E2M1), rhs_scale=s4[:], start=True, stop=False)
-            nc.tensor.matmul_mx(out=acc[:], lhsT=codes.bitcast(E5M2), lhsT_scale=scales,
-                                rhs=w8[:].bitcast(E4M3), rhs_scale=s8[:], start=False, stop=True)
-            return acc
+        def load_weights(h):
+            words = w8_words[0].rearrange("p n t -> p (n t)")
+            nc.sync.dma_start(w8[h][:].bitcast(I32), words[:, 2 * N * h : 2 * N * (h + 1)].bitcast(I32))
+            nc.sync.dma_start(w4[h][:].bitcast(I32), w4_words[0, :, N * h : N * (h + 1)].bitcast(I32))
 
-        def product_by_row(nb, bank, codes, scales):
-            acc = psum.tile([P, HALF], F32, name=f"row{nb}", tag=bank)
+        def load_gain(a, b):
+            nc.sync.dma_start(gain[:, a:b], wgo[:, a:b])
+
+        def weave(copy, i, a, b):
+            first = spans[i][0]
+            loaded = max(start for start in raw if start <= first)
+            source = raw[loaded][:, :, first - loaded + a : first - loaded + b]
+            copy(out=woven[i][:, a:b, :].rearrange("p (c i) t -> p c t i", i=4),
+                 in_=source.rearrange("p t (c i) -> p c t i", i=4))
+
+        def quantise(i):
+            a, b = spans[i]
+            nc.vector.quantize_mx(out=codes[:, a:b].bitcast(E5M2), scales=scales[:, a:b],
+                                  in_=woven[i][:].rearrange("p c t -> p (c t)"))
+
+        def product(nb, a, b, bank):
+            acc = psum.tile([P, BANK], F32, name=f"acc{nb}_{a}", tag=f"bank{bank}")
             cols = slice(nb * P, (nb + 1) * P)
-            nc.tensor.matmul_mx(out=acc[:], lhsT=w4[:, 2 * nb * P : 2 * (nb + 1) * P].bitcast(E2M1), lhsT_scale=s4[:, cols],
-                                rhs=codes[:].bitcast(E5M2), rhs_scale=scales[:], start=True, stop=False)
-            nc.tensor.matmul_mx(out=acc[:], lhsT=w8[:, cols].bitcast(E4M3), lhsT_scale=s8[:, cols],
-                                rhs=codes[:].bitcast(E5M2), rhs_scale=scales[:], start=False, stop=True)
-            return acc
-
-        def turn(by_token, name, bank):
-            count = by_token.shape[1] // P
-            turned = psum.tile([P, count, P], F32, name=f"turned_{name}", tag=bank)
-            for i in range(count):
-                nc.tensor.transpose(turned[:, i, :], by_token[:, i * P : (i + 1) * P], ident[:])
-            return turned
+            h, c = divmod(nb, 2)
+            start = a
+            while start < b:
+                width = max(w for w in (128, 256, 512) if w <= b - start)
+                tokens = slice(start, start + width)
+                part = acc[:, start - a : start - a + width]
+                nc.tensor.matmul_mx(out=part, lhsT=w8[h][:, c * P : (c + 1) * P].bitcast(E4M3), lhsT_scale=s8[:, cols],
+                                    rhs=codes[:, tokens].bitcast(E5M2), rhs_scale=scales[:, tokens], start=True, stop=False)
+                nc.tensor.matmul_mx(out=part, lhsT=w4[h][:, 2 * c * P : 2 * (c + 1) * P].bitcast(E2M1), lhsT_scale=s4[:, cols],
+                                    rhs=codes[:, tokens].bitcast(E5M2), rhs_scale=scales[:, tokens], start=False, stop=True)
+                start += width
+            return acc[:, : b - a]
 
         def window(nb, a, b):
-            return pages[nb][:].indirect(offsets[:, a // 16 : b // 16])
+            return pages[nb % 3][:].indirect(offsets[:, a // 16 : b // 16])
 
-        def scatter_block(nb, dx, a):
-            nc.vector.tensor_tensor(out=window(nb, a, a + P), in0=dx, in1=zeros[:], op=add)
+        def empty(nb, a, b, bank, over=None, slot=0):
+            if over is None:
+                dx[nb, a] = keep.tile([P, b - a], F32, name=f"dx{nb}_{a}")
+            else:
+                dx[nb, a] = shared.tile([P, b - a], F32, name=f"dx{nb}_{a}", align_bytes=64, offset=PAGE_BYTES + 16 * over + 1024 * slot)
+            for first in range(a, b, BANK):
+                last = min(b, first + BANK)
+                nc.scalar.copy(out=dx[nb, a][:, first - a : last - a], in_=product(nb, first, last, bank + (first - a) // BANK))
 
-        def load_gain_column(queue, block):
-            with nc.allow_non_contiguous_dma(reason="one weight a partition"):
-                queue.dma_start(columns[block][:], wgo[0, block * P : (block + 1) * P].rearrange("(b p) -> p b", p=P))
+        def scatter(nb, a, b):
+            nc.vector.tensor_tensor(out=window(nb, a, b), in0=dx[nb, a][:], in1=gain[:, a:b], op=mult)
 
-        nc.gpsimd.memset(s8[:].bitcast(I32), 0)
-        load_scale_rows(nc.sync, s4, w4_scales, 0)
-        load_scale_rows(nc.sync, s4, w4_scales, 1)
-        load_scale_rows(nc.sync, s4, w4_scales, 2)
-        nc.sync.dma_start(raw0[:], dy_rows[:, :, :P])
-        load_scale_rows(nc.sync, s4, w4_scales, 3)
-        nc.sync.dma_start(w4[:].bitcast(I32), w4_words[0].bitcast(I32))
-        nc.sync.dma_start(w8[:].bitcast(I32), w8_words[0].rearrange("p n t -> p (n t)").bitcast(I32))
-        load_scale_rows(nc.sync, s8, w8_scales, 0)
-        load_scale_rows(nc.sync, s8, w8_scales, 1)
-        load_scale_rows(nc.sync, s8, w8_scales, 2)
-        load_scale_rows(nc.sync, s8, w8_scales, 3)
-        load_gain_column(nc.sync, 0)
-        nc.sync.dma_start(raw1[:], dy_rows[:, :, P : 2 * P])
+        def store(nb):
+            nc.sync.dma_start(out[nb * P : (nb + 1) * P, :], pages[nb % 3][:])
+
+        nc.vector.memset(planes[:].bitcast(I32), 0)
         nc.sync.dma_start(offsets[:], offs)
-        nc.sync.dma_start(raw23[:], dy_rows[:, :, 2 * P : HALF])
-        load_gain_column(nc.sync, 1)
-        nc.sync.dma_start(raw_late[:], dy_rows[:, :, HALF:])
-        load_gain_column(nc.sync, 2)
-        load_gain_column(nc.sync, 3)
-        nc.sync.dma_start(gain[:], wgo[:, HALF:])
+        load_dy(0)
+        load_first_scale_rows(nc.scalar, s4, w4_scales)
+        load_first_scale_rows(nc.sync, s8, w8_scales)
+        load_weights(0)
+        load_last_scale_rows(nc.sync, s8, w8_scales)
+        load_last_scale_rows(nc.sync, s4, w4_scales)
+        load_gain(0, P)
+        load_gain(P, 384)
+        load_weights(1)
+        load_dy(1)
+        load_dy(2)
+        load_gain(384, 640)
+        load_dy(3)
+        load_dy(4)
+        load_gain(640, J)
 
-        make_identity(nc, ident[:])
-        nc.scalar.activation(out=zeros[:], in_=ident[:], func=copy_fn, scale=0.0)
-        for page in pages:
-            nc.vector.memset(page[:].bitcast(I32), 0)
-
-
-        woven0 = chain.tile([P, P, 4], BF16, name="woven0", align_bytes=64, offset=AT_WOVEN0)
-        weave(nc.vector.tensor_copy, woven0[:, :VECTOR_SHARE, :], raw0[:, :, :VECTOR_SHARE])
-        weave(nc.scalar.copy, woven0[:, VECTOR_SHARE:, :], raw0[:, :, VECTOR_SHARE:])
-        codes0, scales0 = quantise(woven0, P, "b0")
-        pages.append(chain.tile([P, T], F32, name="page2", align_bytes=64, offset=AT_PAGE2))
-        nc.vector.memset(pages[2][:].bitcast(I32), 0)
-
-        acc = product_by_token("0", "acc", codes0[:], scales0[:])
-        woven1 = chain.tile([P, P, 4], BF16, name="woven1", align_bytes=64, offset=AT_WOVEN1)
-        weave(nc.vector.tensor_copy, woven1[:], raw1[:])
-        codes1, scales1 = quantise(woven1, P, "b1")
-        pages.append(chain.tile([P, T], F32, name="page3", align_bytes=64, offset=AT_PAGE3))
-        nc.gpsimd.memset(pages[3][:], 0.0)
-        first = keep.tile([P, P], F32, name="first")
-        nc.scalar.activation(out=first[:], in_=acc[:, :P], func=copy_fn, scale=columns[0][:, 0:1])
-        turned_a = turn(first[:], "0a", "turn0")
-        rest = chain.tile([P, 3 * P], F32, name="rest", align_bytes=64, offset=AT_REST)
-        nc.scalar.activation(out=rest[:], in_=acc[:, P:], func=copy_fn, scale=columns[0][:, 0:1])
-        dx_a = keep.tile([P, P], F32, name="dx_a")
-        nc.vector.tensor_copy(out=dx_a[:], in_=turned_a[:, 0, :])
-        scatter_block(0, dx_a[:], 0)
-        turned_b = turn(rest[:, :P], "0b", "turn2")
-        turned_cd = turn(rest[:, P:], "0cd", "turn1")
-        dx_b = keep.tile([P, P], F32, name="dx_b")
-        nc.scalar.copy(out=dx_b[:], in_=turned_b[:, 0, :])
-        scatter_block(1, dx_b[:], 0)
-        dx_c = keep.tile([P, P], F32, name="dx_c")
-        nc.scalar.copy(out=dx_c[:], in_=turned_cd[:, 0, :])
-        scatter_block(2, dx_c[:], 0)
-        woven2 = chain.tile([P, P, 4], BF16, name="woven2", align_bytes=64, offset=AT_REST)
-        weave(nc.scalar.copy, woven2[:], raw23[:, :, :P])
-        codes2, scales2 = quantise(woven2, P, "b2")
-        dx_d = keep.tile([P, P], F32, name="dx_d")
-        nc.scalar.copy(out=dx_d[:], in_=turned_cd[:, 1, :])
-        scatter_block(3, dx_d[:], 0)
-
-        acc = product_by_token("1", "acc", codes1[:], scales1[:])
-        by_token1 = chain.tile([P, N], F32, name="by_token1", align_bytes=64, offset=AT_BY_TOKEN1)
-        dx1_ab = keep.tile([P, 2, P], F32, name="dx1_ab")
-        nc.scalar.activation(out=by_token1[:, :P], in_=acc[:, :P], func=copy_fn, scale=columns[1][:, 0:1])
-        turned_a = turn(by_token1[:, :P], "1a", "turn0")
-        nc.scalar.activation(out=by_token1[:, P:], in_=acc[:, P:], func=copy_fn, scale=columns[1][:, 0:1])
-        turned_b = turn(by_token1[:, P : 2 * P], "1b", "turn2")
-        turned_cd = turn(by_token1[:, 2 * P :], "1cd", "turn1")
-        for nb, turned in enumerate((turned_a, turned_b)):
-            nc.scalar.copy(out=dx1_ab[:, nb, :], in_=turned[:, 0, :])
-            scatter_block(nb, dx1_ab[:, nb, :], P)
-        woven3 = chain.tile([P, P, 4], BF16, name="woven3", align_bytes=64, offset=AT_BY_TOKEN1)
-        weave(nc.scalar.copy, woven3[:], raw23[:, :, P:])
-        codes3, scales3 = quantise(woven3, P, "b3")
-        dx1_cd = chain.tile([P, 2, P], F32, name="dx1_cd", align_bytes=64, offset=AT_RAW23 + 2 * WOVEN_BYTES)
-        nc.scalar.copy(out=dx1_cd[:], in_=turned_cd[:])
-        for nb in (2, 3):
-            scatter_block(nb, dx1_cd[:, nb - 2, :], P)
-
-        acc = product_by_token("2", "acc", codes2[:], scales2[:])
-        by_token2 = chain.tile([P, N], F32, name="by_token2", align_bytes=64, offset=AT_BY_TOKEN2)
-        halves = []
-        for h in range(2):
-            cols = slice(2 * h * P, 2 * (h + 1) * P)
-            nc.scalar.activation(out=by_token2[:, cols], in_=acc[:, cols], func=copy_fn, scale=columns[2][:, 0:1])
-            halves.append(turn(by_token2[:, cols], f"2{h}", ("turn0", "turn1")[h]))
-        dx2 = keep.tile([P, 4, P], F32, name="dx2")
-        for h in range(2):
-            nc.scalar.copy(out=dx2[:, 2 * h : 2 * h + 2, :], in_=halves[h][:])
-            for nb in (2 * h, 2 * h + 1):
-                scatter_block(nb, dx2[:, nb, :], 2 * P)
-        late = (keep.tile([P, HALF], U32, name="codes_late", align_bytes=64),
-                keep.tile([P, HALF], U8, name="scales_late", align_bytes=64))
-        for part, at in enumerate((AT_RAW23, AT_BY_TOKEN2)):
-            woven = chain.tile([P, 2 * P, 4], BF16, name=f"woven_late{part}", align_bytes=64, offset=at)
-            for piece in range(2):
-                first_col = (2 * part + piece) * P
-                weave(nc.scalar.copy, woven[:, piece * P : (piece + 1) * P, :], raw_late[:, :, first_col : first_col + P])
-            cols = slice(2 * part * P, 2 * (part + 1) * P)
-            nc.vector.quantize_mx(out=late[0][:, cols].bitcast(E5M2), scales=late[1][:, cols],
-                                  in_=woven[:].rearrange("p c t -> p (c t)"))
-        acc = product_by_token("3", "acc", codes3[:], scales3[:])
-        by_token3 = chain.tile([P, N], F32, name="by_token3", align_bytes=64, offset=AT_RAW_LATE)
-        halves = []
-        for h in range(2):
-            cols = slice(2 * h * P, 2 * (h + 1) * P)
-            nc.scalar.activation(out=by_token3[:, cols], in_=acc[:, cols], func=copy_fn, scale=columns[3][:, 0:1])
-            halves.append(turn(by_token3[:, cols], f"3{h}", ("turn2", "turn0")[h]))
-        dx3 = keep.tile([P, 4, P], F32, name="dx3")
-        for h in range(2):
-            nc.scalar.copy(out=dx3[:, 2 * h : 2 * h + 2, :], in_=halves[h][:])
-            for nb in (2 * h, 2 * h + 1):
-                scatter_block(nb, dx3[:, nb, :], 3 * P)
-
-        for nb in range(4):
-            tail = keep.tile([P, HALF], F32, name=f"tail{nb}")
-            nc.scalar.copy(out=tail[:], in_=product_by_row(nb, "turn0", *late)[:])
-            nc.vector.tensor_tensor(out=window(nb, HALF, J), in0=tail[:], in1=gain[:], op=mult)
-            nc.sync.dma_start(out[nb * P : (nb + 1) * P, :], pages[nb][:])
+        nc.vector.memset(zeros[:], 0.0)
+        nc.vector.memset(pages[0][:, : T - 1], 0.0)
+        nc.vector.memset(pages[0][:, T - 1 :], 0.0)
+        nc.gpsimd.memset(pages[1][:], 0.0)
+        for i in range(2):
+            weave(nc.vector.tensor_copy, i, 0, VECTOR_SHARE)
+            weave(nc.scalar.copy, i, VECTOR_SHARE, P)
+        quantise(0)
+        quantise(1)
+        pages.append(shared.tile([P, T], F32, name="page2", align_bytes=64, offset=0))
+        nc.gpsimd.memset(pages[2][:], 0.0)
+        first_dx = shared.tile([P, P], F32, name="first_dx", align_bytes=64, offset=AT_FIRST_DX)
+        nc.vector.tensor_tensor(out=first_dx[:], in0=product(0, 0, P, 0), in1=gain[:, :P], op=mult)
+        empty(1, 0, 256, 1)
+        nc.vector.tensor_tensor(out=window(0, 0, P), in0=first_dx[:], in1=zeros[:], op=add)
+        woven[2] = shared.tile([P, P, 4], BF16, name="woven256", align_bytes=64, offset=AT_FIRST_DX)
+        weave(nc.scalar.copy, 2, 0, P)
+        empty(2, 0, 256, 2, over=256)
+        scatter(1, 0, 256)
+        quantise(2)
+        weave(nc.scalar.copy, 3, 0, P)
+        scatter(2, 0, 256)
+        empty(0, 128, 384, 3, over=384)
+        quantise(3)
+        weave(nc.scalar.copy, 4, 0, 256)
+        scatter(0, 128, 384)
+        empty(1, 256, 512, 4, over=512)
+        quantise(4)
+        weave(nc.scalar.copy, 5, 0, 256)
+        scatter(1, 256, 512)
+        empty(2, 256, 512, 5, over=768)
+        quantise(5)
+        scatter(2, 256, 512)
+        empty(0, 384, 640, 6, over=768, slot=1)
+        empty(2, 512, 768, 7, over=768, slot=2)
+        scatter(0, 384, 640)
+        empty(0, 640, J, 0)
+        scatter(2, 512, 768)
+        empty(1, 512, J, 1)
+        scatter(0, 640, J)
+        store(0)
+        empty(2, 768, J, 2)
+        scatter(1, 512, J)
+        store(1)
+        empty(3, 0, J, 3)
+        scatter(2, 768, J)
+        store(2)
+        scatter(3, 0, J)
+        store(3)

@@ -113,7 +113,7 @@ def tile_list_embg_res_none_kernel(tc, dy, w4_words, w4_scales, w8_words, w8_sca
         def store(nb):
             nc.sync.dma_start(out[nb * P : (nb + 1) * P, :], pages[nb % 3][:])
 
-        nc.vector.memset(planes[:].bitcast(I32), 0)
+        nc.gpsimd.memset(planes[:].bitcast(I32), 0)
         nc.sync.dma_start(offsets[:], offs)
         load_dy(0)
         load_first_scale_rows(nc.scalar, s4, w4_scales)
@@ -131,10 +131,10 @@ def tile_list_embg_res_none_kernel(tc, dy, w4_words, w4_scales, w8_words, w8_sca
         load_dy(4)
         load_gain(640, J)
 
-        nc.vector.memset(zeros[:], 0.0)
         nc.vector.memset(pages[0][:, : T - 1], 0.0)
         nc.vector.memset(pages[0][:, T - 1 :], 0.0)
         nc.gpsimd.memset(pages[1][:], 0.0)
+        nc.gpsimd.memset(zeros[:], 0.0)
         for i in range(2):
             weave(nc.vector.tensor_copy, i, 0, VECTOR_SHARE)
             weave(nc.scalar.copy, i, VECTOR_SHARE, P)

@@ -17,8 +17,7 @@ P = 128
 BANK = 512
 REPEATED_ROWS = 14
 VECTOR_SHARE = 80
-PAGE_BYTES = 4 * T
-AT_FIRST_DX = PAGE_BYTES + 16 * J
+AT_FIRST_DX = 16 * J
 
 
 def tile_list_embg_res_none_kernel(tc, dy, w4_words, w4_scales, w8_words, w8_scales, wgo, offs, out):
@@ -40,13 +39,12 @@ def tile_list_embg_res_none_kernel(tc, dy, w4_words, w4_scales, w8_words, w8_sca
         zeros = keep.tile([P, P], F32, name="zeros")
         codes = keep.tile([P, J], U32, name="codes", align_bytes=64)
         scales = keep.tile([P, J], U8, name="scales", align_bytes=64)
-        pages = [keep.tile([P, T], F32, name=f"page{w}") for w in range(2)]
+        pages = [keep.tile([P, T], F32, name=f"page{w}") for w in range(3)]
         spans = ((0, 128), (128, 256), (256, 384), (384, 512), (512, 768), (768, 1024))
         loads = ((0, 256), (256, 384), (384, 512), (512, 768), (768, 1024))
-        raw = {a: shared.tile([P, 4, b - a], F32, name=f"raw{a}", align_bytes=64, offset=PAGE_BYTES + 16 * a) for a, b in loads}
+        raw = {a: shared.tile([P, 4, b - a], F32, name=f"raw{a}", align_bytes=64, offset=16 * a) for a, b in loads}
         dx = {}
-        woven = {i: keep.tile([P, b - a, 4], BF16, name=f"woven{a}", align_bytes=64) for i, (a, b) in enumerate(spans) if i not in (1, 2)}
-        woven[1] = shared.tile([P, P, 4], BF16, name="woven128", align_bytes=64, offset=0)
+        woven = {i: keep.tile([P, b - a, 4], BF16, name=f"woven{a}", align_bytes=64) for i, (a, b) in enumerate(spans) if i != 2}
 
         def load_first_scale_rows(queue, plane, rows):
             source = rows[0, :REPEATED_ROWS, :].bitcast(I32).partition_broadcast(7)
@@ -102,7 +100,7 @@ def tile_list_embg_res_none_kernel(tc, dy, w4_words, w4_scales, w8_words, w8_sca
             if over is None:
                 dx[nb, a] = keep.tile([P, b - a], F32, name=f"dx{nb}_{a}")
             else:
-                dx[nb, a] = shared.tile([P, b - a], F32, name=f"dx{nb}_{a}", align_bytes=64, offset=PAGE_BYTES + 16 * over + 1024 * slot)
+                dx[nb, a] = shared.tile([P, b - a], F32, name=f"dx{nb}_{a}", align_bytes=64, offset=16 * over + 1024 * slot)
             for first in range(a, b, BANK):
                 last = min(b, first + BANK)
                 nc.scalar.copy(out=dx[nb, a][:, first - a : last - a], in_=product(nb, first, last, bank + (first - a) // BANK))
@@ -113,7 +111,7 @@ def tile_list_embg_res_none_kernel(tc, dy, w4_words, w4_scales, w8_words, w8_sca
         def store(nb):
             nc.sync.dma_start(out[nb * P : (nb + 1) * P, :], pages[nb % 3][:])
 
-        nc.gpsimd.memset(planes[:].bitcast(I32), 0)
+        nc.vector.memset(planes[:].bitcast(I32), 0)
         nc.sync.dma_start(offsets[:], offs)
         load_dy(0)
         load_first_scale_rows(nc.scalar, s4, w4_scales)
@@ -131,17 +129,14 @@ def tile_list_embg_res_none_kernel(tc, dy, w4_words, w4_scales, w8_words, w8_sca
         load_dy(4)
         load_gain(640, J)
 
-        nc.vector.memset(pages[0][:, : T - 1], 0.0)
-        nc.vector.memset(pages[0][:, T - 1 :], 0.0)
-        nc.gpsimd.memset(pages[1][:], 0.0)
-        nc.gpsimd.memset(zeros[:], 0.0)
+        nc.vector.memset(zeros[:], 0.0)
+        for page in pages:
+            nc.vector.memset(page[:].bitcast(I32), 0)
         for i in range(2):
             weave(nc.vector.tensor_copy, i, 0, VECTOR_SHARE)
             weave(nc.scalar.copy, i, VECTOR_SHARE, P)
         quantise(0)
         quantise(1)
-        pages.append(shared.tile([P, T], F32, name="page2", align_bytes=64, offset=0))
-        nc.gpsimd.memset(pages[2][:], 0.0)
         first_dx = shared.tile([P, P], F32, name="first_dx", align_bytes=64, offset=AT_FIRST_DX)
         nc.vector.tensor_tensor(out=first_dx[:], in0=product(0, 0, P, 0), in1=gain[:, :P], op=mult)
         empty(1, 0, 256, 1)

@@ -16,7 +16,6 @@ E2M1 = mybir.dt.float4_e2m1fn_x4
 P = 128
 BANK = 512
 REPEATED_ROWS = 14
-VECTOR_SHARE = 80
 AT_FIRST_DX = 16 * J
 
 
@@ -36,7 +35,6 @@ def tile_list_embg_res_none_kernel(tc, dy, w4_words, w4_scales, w8_words, w8_sca
         planes = keep.tile([P, 2 * N], U8, name="planes", align_bytes=64)
         s4, s8 = planes[:, :N], planes[:, N:]
         gain = keep.tile([P, J], F32, name="gain")
-        zeros = keep.tile([P, P], F32, name="zeros")
         codes = keep.tile([P, J], U32, name="codes", align_bytes=64)
         scales = keep.tile([P, J], U8, name="scales", align_bytes=64)
         pages = [keep.tile([P, T], F32, name=f"page{w}") for w in range(3)]
@@ -86,10 +84,11 @@ def tile_list_embg_res_none_kernel(tc, dy, w4_words, w4_scales, w8_words, w8_sca
                 width = max(w for w in (128, 256, 512) if w <= b - start)
                 tokens = slice(start, start + width)
                 part = acc[:, start - a : start - a + width]
-                nc.tensor.matmul_mx(out=part, lhsT=w8[h][:, c * P : (c + 1) * P].bitcast(E4M3), lhsT_scale=s8[:, cols],
-                                    rhs=codes[:, tokens].bitcast(E5M2), rhs_scale=scales[:, tokens], start=True, stop=False)
-                nc.tensor.matmul_mx(out=part, lhsT=w4[h][:, 2 * c * P : 2 * (c + 1) * P].bitcast(E2M1), lhsT_scale=s4[:, cols],
-                                    rhs=codes[:, tokens].bitcast(E5M2), rhs_scale=scales[:, tokens], start=False, stop=True)
+                tiers = [(w4[h][:, 2 * c * P : 2 * (c + 1) * P].bitcast(E2M1), s4[:, cols]),
+                         (w8[h][:, c * P : (c + 1) * P].bitcast(E4M3), s8[:, cols])]
+                for i, (words, plane) in enumerate(reversed(tiers) if (nb, a) == (0, 0) else tiers):
+                    nc.tensor.matmul_mx(out=part, lhsT=words, lhsT_scale=plane, rhs=codes[:, tokens].bitcast(E5M2),
+                                        rhs_scale=scales[:, tokens], start=i == 0, stop=i == 1)
                 start += width
             return acc[:, : b - a]
 
@@ -114,11 +113,10 @@ def tile_list_embg_res_none_kernel(tc, dy, w4_words, w4_scales, w8_words, w8_sca
         nc.vector.memset(planes[:].bitcast(I32), 0)
         nc.sync.dma_start(offsets[:], offs)
         load_dy(0)
-        load_first_scale_rows(nc.scalar, s4, w4_scales)
-        load_first_scale_rows(nc.sync, s8, w8_scales)
         load_weights(0)
-        load_last_scale_rows(nc.sync, s8, w8_scales)
-        load_last_scale_rows(nc.sync, s4, w4_scales)
+        for plane, rows in ((s8, w8_scales), (s4, w4_scales)):
+            load_first_scale_rows(nc.sync, plane, rows)
+            load_last_scale_rows(nc.sync, plane, rows)
         load_gain(0, P)
         load_gain(P, 384)
         load_weights(1)
@@ -129,18 +127,15 @@ def tile_list_embg_res_none_kernel(tc, dy, w4_words, w4_scales, w8_words, w8_sca
         load_dy(4)
         load_gain(640, J)
 
-        nc.vector.memset(zeros[:], 0.0)
         for page in pages:
             nc.vector.memset(page[:].bitcast(I32), 0)
         for i in range(2):
-            weave(nc.vector.tensor_copy, i, 0, VECTOR_SHARE)
-            weave(nc.scalar.copy, i, VECTOR_SHARE, P)
-        quantise(0)
-        quantise(1)
+            weave(nc.scalar.copy, i, 0, P)
+            quantise(i)
         first_dx = shared.tile([P, P], F32, name="first_dx", align_bytes=64, offset=AT_FIRST_DX)
         nc.vector.tensor_tensor(out=first_dx[:], in0=product(0, 0, P, 0), in1=gain[:, :P], op=mult)
         empty(1, 0, 256, 1)
-        nc.vector.tensor_tensor(out=window(0, 0, P), in0=first_dx[:], in1=zeros[:], op=add)
+        nc.vector.tensor_tensor(out=window(0, 0, P), in0=first_dx[:], in1=pages[2][:, :P], op=add)
         woven[2] = shared.tile([P, P, 4], BF16, name="woven256", align_bytes=64, offset=AT_FIRST_DX)
         weave(nc.scalar.copy, 2, 0, P)
         empty(2, 0, 256, 2, over=256)
@@ -170,7 +165,7 @@ def tile_list_embg_res_none_kernel(tc, dy, w4_words, w4_scales, w8_words, w8_sca
         empty(2, 768, J, 2)
         scatter(1, 512, J)
         store(1)
-        empty(3, 0, J, 3)
+        empty(3, 0, J, 6)
         scatter(2, 768, J)
         store(2)
         scatter(3, 0, J)

@@ -16,12 +16,13 @@ E2M1 = mybir.dt.float4_e2m1fn_x4
 P = 128
 BANK = 512
 REPEATED_ROWS = 14
-AT_FIRST_DX = 16 * J
+VECTOR_SHARE = 80
+AT_PAGE2 = 16 * J
 
 
 def tile_list_embg_res_none_kernel(tc, dy, w4_words, w4_scales, w8_words, w8_scales, wgo, offs, out):
     nc = tc.nc
-    mult, add = mybir.AluOpType.mult, mybir.AluOpType.add
+    mult = mybir.AluOpType.mult
     dy_rows = dy.rearrange("(p t) j -> p t j", t=4)
 
     with (
@@ -30,42 +31,41 @@ def tile_list_embg_res_none_kernel(tc, dy, w4_words, w4_scales, w8_words, w8_sca
         tc.psum_pool(name="psum", bufs=1) as psum,
     ):
         offsets = keep.tile([P, J // 16], U16, name="offsets")
-        w4 = [keep.tile([P, N], U8, name=f"w4_{h}", align_bytes=64) for h in range(2)]
-        w8 = [keep.tile([P, N // 2], U32, name=f"w8_{h}", align_bytes=64) for h in range(2)]
+        w4 = keep.tile([P, 2 * N], U8, name="w4", align_bytes=64)
+        w8 = keep.tile([P, N], U32, name="w8", align_bytes=64)
         planes = keep.tile([P, 2 * N], U8, name="planes", align_bytes=64)
         s4, s8 = planes[:, :N], planes[:, N:]
         gain = keep.tile([P, J], F32, name="gain")
         codes = keep.tile([P, J], U32, name="codes", align_bytes=64)
         scales = keep.tile([P, J], U8, name="scales", align_bytes=64)
-        pages = [keep.tile([P, T], F32, name=f"page{w}") for w in range(3)]
-        spans = ((0, 128), (128, 256), (256, 384), (384, 512), (512, 768), (768, 1024))
-        loads = ((0, 256), (256, 384), (384, 512), (512, 768), (768, 1024))
+        pages = [keep.tile([P, T], F32, name=f"page{w}") for w in range(2)]
+        spans = ((0, 128), (128, 256), (256, 512), (512, 1024))
+        loads = ((0, 256), (256, 512), (512, 768), (768, 1024))
         raw = {a: shared.tile([P, 4, b - a], F32, name=f"raw{a}", align_bytes=64, offset=16 * a) for a, b in loads}
         dx = {}
-        woven = {i: keep.tile([P, b - a, 4], BF16, name=f"woven{a}", align_bytes=64) for i, (a, b) in enumerate(spans) if i != 2}
+        woven = {i: keep.tile([P, b - a, 4], BF16, name=f"woven{a}", align_bytes=64) for i, (a, b) in enumerate(spans) if i != 1}
+        woven[1] = shared.tile([P, P, 4], BF16, name="woven128", align_bytes=64, offset=AT_PAGE2)
 
-        def load_first_scale_rows(queue, plane, rows):
-            source = rows[0, :REPEATED_ROWS, :].bitcast(I32).partition_broadcast(7)
-            queue.dma_start(plane[: 7 * REPEATED_ROWS, :].bitcast(I32), source)
-
-        def load_last_scale_rows(queue, plane, rows):
-            queue.dma_start(plane[98:100, :].bitcast(I32), rows[0, REPEATED_ROWS:, :].bitcast(I32))
+        def load_repeated_scale_rows(a, b):
+            for plane, rows in ((s8, w8_scales), (s4, w4_scales)):
+                source = rows[0, :REPEATED_ROWS, a:b].bitcast(I32).partition_broadcast(7)
+                nc.sync.dma_start(plane[: 7 * REPEATED_ROWS, a:b].bitcast(I32), source)
 
         def load_dy(i):
             a, b = loads[i]
             nc.sync.dma_start(raw[a][:], dy_rows[:, :, a:b])
 
-        def load_weights(h):
+        def load_weights(a, b):
             words = w8_words[0].rearrange("p n t -> p (n t)")
-            nc.sync.dma_start(w8[h][:].bitcast(I32), words[:, 2 * N * h : 2 * N * (h + 1)].bitcast(I32))
-            nc.sync.dma_start(w4[h][:].bitcast(I32), w4_words[0, :, N * h : N * (h + 1)].bitcast(I32))
+            nc.sync.dma_start(w8[:, a:b].bitcast(I32), words[:, 4 * a : 4 * b].bitcast(I32))
+            nc.sync.dma_start(w4[:, 2 * a : 2 * b].bitcast(I32), w4_words[0, :, 2 * a : 2 * b].bitcast(I32))
 
         def load_gain(a, b):
             nc.sync.dma_start(gain[:, a:b], wgo[:, a:b])
 
         def weave(copy, i, a, b):
             first = spans[i][0]
-            loaded = max(start for start in raw if start <= first)
+            loaded = max(start for start in raw if start <= first + a)
             source = raw[loaded][:, :, first - loaded + a : first - loaded + b]
             copy(out=woven[i][:, a:b, :].rearrange("p (c i) t -> p c t i", i=4),
                  in_=source.rearrange("p t (c i) -> p c t i", i=4))
@@ -78,15 +78,14 @@ def tile_list_embg_res_none_kernel(tc, dy, w4_words, w4_scales, w8_words, w8_sca
         def product(nb, a, b, bank):
             acc = psum.tile([P, BANK], F32, name=f"acc{nb}_{a}", tag=f"bank{bank}")
             cols = slice(nb * P, (nb + 1) * P)
-            h, c = divmod(nb, 2)
             start = a
             while start < b:
                 width = max(w for w in (128, 256, 512) if w <= b - start)
                 tokens = slice(start, start + width)
                 part = acc[:, start - a : start - a + width]
-                tiers = [(w4[h][:, 2 * c * P : 2 * (c + 1) * P].bitcast(E2M1), s4[:, cols]),
-                         (w8[h][:, c * P : (c + 1) * P].bitcast(E4M3), s8[:, cols])]
-                for i, (words, plane) in enumerate(reversed(tiers) if (nb, a) == (0, 0) else tiers):
+                tiers = [(w4[:, 2 * nb * P : 2 * (nb + 1) * P].bitcast(E2M1), s4[:, cols]),
+                         (w8[:, cols].bitcast(E4M3), s8[:, cols])]
+                for i, (words, plane) in enumerate(reversed(tiers) if nb == 0 and a < 256 else tiers):
                     nc.tensor.matmul_mx(out=part, lhsT=words, lhsT_scale=plane, rhs=codes[:, tokens].bitcast(E5M2),
                                         rhs_scale=scales[:, tokens], start=i == 0, stop=i == 1)
                 start += width
@@ -95,14 +94,14 @@ def tile_list_embg_res_none_kernel(tc, dy, w4_words, w4_scales, w8_words, w8_sca
         def window(nb, a, b):
             return pages[nb % 3][:].indirect(offsets[:, a // 16 : b // 16])
 
-        def empty(nb, a, b, bank, over=None, slot=0):
+        def empty(nb, a, b, bank, over=None, slot=0, step=BANK):
             if over is None:
                 dx[nb, a] = keep.tile([P, b - a], F32, name=f"dx{nb}_{a}")
             else:
                 dx[nb, a] = shared.tile([P, b - a], F32, name=f"dx{nb}_{a}", align_bytes=64, offset=16 * over + 1024 * slot)
-            for first in range(a, b, BANK):
-                last = min(b, first + BANK)
-                nc.scalar.copy(out=dx[nb, a][:, first - a : last - a], in_=product(nb, first, last, bank + (first - a) // BANK))
+            for i, first in enumerate(range(a, b, step)):
+                last = min(b, first + step)
+                nc.scalar.copy(out=dx[nb, a][:, first - a : last - a], in_=product(nb, first, last, bank + i))
 
         def scatter(nb, a, b):
             nc.vector.tensor_tensor(out=window(nb, a, b), in0=dx[nb, a][:], in1=gain[:, a:b], op=mult)
@@ -111,62 +110,48 @@ def tile_list_embg_res_none_kernel(tc, dy, w4_words, w4_scales, w8_words, w8_sca
             nc.sync.dma_start(out[nb * P : (nb + 1) * P, :], pages[nb % 3][:])
 
         nc.vector.memset(planes[:].bitcast(I32), 0)
-        nc.sync.dma_start(offsets[:], offs)
         load_dy(0)
-        load_weights(0)
+        load_weights(0, P)
+        load_repeated_scale_rows(0, 2 * P)
         for plane, rows in ((s8, w8_scales), (s4, w4_scales)):
-            load_first_scale_rows(nc.sync, plane, rows)
-            load_last_scale_rows(nc.sync, plane, rows)
-        load_gain(0, P)
-        load_gain(P, 384)
-        load_weights(1)
+            nc.scalar.dma_start(plane[98:100, :].bitcast(I32), rows[0, REPEATED_ROWS:, :].bitcast(I32))
+        load_gain(0, 256)
+        nc.sync.dma_start(offsets[:], offs)
+        load_weights(P, N)
         load_dy(1)
+        load_repeated_scale_rows(2 * P, N)
         load_dy(2)
-        load_gain(384, 640)
+        load_gain(256, 512)
         load_dy(3)
-        load_dy(4)
-        load_gain(640, J)
+        load_gain(512, J)
 
         for page in pages:
             nc.vector.memset(page[:].bitcast(I32), 0)
         for i in range(2):
-            weave(nc.scalar.copy, i, 0, P)
-            quantise(i)
-        first_dx = shared.tile([P, P], F32, name="first_dx", align_bytes=64, offset=AT_FIRST_DX)
-        nc.vector.tensor_tensor(out=first_dx[:], in0=product(0, 0, P, 0), in1=gain[:, :P], op=mult)
-        empty(1, 0, 256, 1)
-        nc.vector.tensor_tensor(out=window(0, 0, P), in0=first_dx[:], in1=pages[2][:, :P], op=add)
-        woven[2] = shared.tile([P, P, 4], BF16, name="woven256", align_bytes=64, offset=AT_FIRST_DX)
-        weave(nc.scalar.copy, 2, 0, P)
-        empty(2, 0, 256, 2, over=256)
+            weave(nc.vector.tensor_copy, i, 0, VECTOR_SHARE)
+            weave(nc.scalar.copy, i, VECTOR_SHARE, P)
+        quantise(0)
+        quantise(1)
+        pages.append(shared.tile([P, T], F32, name="page2", align_bytes=64, offset=AT_PAGE2))
+        nc.vector.memset(pages[2][:].bitcast(I32), 0)
+        empty(0, 0, 256, 0, step=P)
+        empty(1, 0, 256, 2)
+        scatter(0, 0, 256)
+        weave(nc.scalar.copy, 2, 0, 256)
+        empty(2, 0, 256, 3, over=256)
         scatter(1, 0, 256)
         quantise(2)
-        weave(nc.scalar.copy, 3, 0, P)
         scatter(2, 0, 256)
-        empty(0, 128, 384, 3, over=384)
+        empty(0, 256, 512, 3)
+        weave(nc.scalar.copy, 3, 0, 256)
+        weave(nc.scalar.copy, 3, 256, 512)
+        scatter(0, 256, 512)
+        empty(1, 256, 512, 3, over=768)
+        empty(2, 256, 512, 3, over=768, slot=1)
         quantise(3)
-        weave(nc.scalar.copy, 4, 0, 256)
-        scatter(0, 128, 384)
-        empty(1, 256, 512, 4, over=512)
-        quantise(4)
-        weave(nc.scalar.copy, 5, 0, 256)
         scatter(1, 256, 512)
-        empty(2, 256, 512, 5, over=768)
-        quantise(5)
         scatter(2, 256, 512)
-        empty(0, 384, 640, 6, over=768, slot=1)
-        empty(2, 512, 768, 7, over=768, slot=2)
-        scatter(0, 384, 640)
-        empty(0, 640, J, 0)
-        scatter(2, 512, 768)
-        empty(1, 512, J, 1)
-        scatter(0, 640, J)
-        store(0)
-        empty(2, 768, J, 2)
-        scatter(1, 512, J)
-        store(1)
-        empty(3, 0, J, 6)
-        scatter(2, 768, J)
-        store(2)
-        scatter(3, 0, J)
-        store(3)
+        for nb, first, bank in ((0, 512, 5), (1, 512, 6), (2, 512, 7), (3, 0, 3)):
+            empty(nb, first, J, bank)
+            scatter(nb, first, J)
+            store(nb)

import concourse.mybir as mybir

K, N, T, J = 512, 512, 2048, 1024
FLOPS = 2 * 2 * K * N * J

F32 = mybir.dt.float32
BF16 = mybir.dt.bfloat16
I32 = mybir.dt.int32
U32 = mybir.dt.uint32
U16 = mybir.dt.uint16
U8 = mybir.dt.uint8
E5M2 = mybir.dt.float8_e5m2_x4
E4M3 = mybir.dt.float8_e4m3fn_x4
E2M1 = mybir.dt.float4_e2m1fn_x4

P = 128
BANK = 512
REPEATED_ROWS = 14
VECTOR_SHARE = 80
AT_PAGE2 = 16 * J


def tile_list_embg_res_none_kernel(tc, dy, w4_words, w4_scales, w8_words, w8_scales, wgo, offs, out):
    nc = tc.nc
    mult = mybir.AluOpType.mult
    dy_rows = dy.rearrange("(p t) j -> p t j", t=4)

    with (
        tc.tile_pool(name="keep", bufs=1) as keep,
        tc.tile_pool(name="shared", bufs=1) as shared,
        tc.psum_pool(name="psum", bufs=1) as psum,
    ):
        offsets = keep.tile([P, J // 16], U16, name="offsets")
        w4 = keep.tile([P, 2 * N], U8, name="w4", align_bytes=64)
        w8 = keep.tile([P, N], U32, name="w8", align_bytes=64)
        planes = keep.tile([P, 2 * N], U8, name="planes", align_bytes=64)
        s4, s8 = planes[:, :N], planes[:, N:]
        gain = keep.tile([P, J], F32, name="gain")
        codes = keep.tile([P, J], U32, name="codes", align_bytes=64)
        scales = keep.tile([P, J], U8, name="scales", align_bytes=64)
        pages = [keep.tile([P, T], F32, name=f"page{w}") for w in range(2)]
        spans = ((0, 128), (128, 256), (256, 512), (512, 1024))
        loads = ((0, 256), (256, 512), (512, 768), (768, 1024))
        raw = {a: shared.tile([P, 4, b - a], F32, name=f"raw{a}", align_bytes=64, offset=16 * a) for a, b in loads}
        dx = {}
        woven = {i: keep.tile([P, b - a, 4], BF16, name=f"woven{a}", align_bytes=64) for i, (a, b) in enumerate(spans) if i != 1}
        woven[1] = shared.tile([P, P, 4], BF16, name="woven128", align_bytes=64, offset=AT_PAGE2)

        def load_repeated_scale_rows(a, b):
            for plane, rows in ((s8, w8_scales), (s4, w4_scales)):
                source = rows[0, :REPEATED_ROWS, a:b].bitcast(I32).partition_broadcast(7)
                nc.sync.dma_start(plane[: 7 * REPEATED_ROWS, a:b].bitcast(I32), source)

        def load_dy(i):
            a, b = loads[i]
            nc.sync.dma_start(raw[a][:], dy_rows[:, :, a:b])

        def load_weights(a, b):
            words = w8_words[0].rearrange("p n t -> p (n t)")
            nc.sync.dma_start(w8[:, a:b].bitcast(I32), words[:, 4 * a : 4 * b].bitcast(I32))
            nc.sync.dma_start(w4[:, 2 * a : 2 * b].bitcast(I32), w4_words[0, :, 2 * a : 2 * b].bitcast(I32))

        def load_gain(a, b):
            nc.sync.dma_start(gain[:, a:b], wgo[:, a:b])

        def weave(copy, i, a, b):
            first = spans[i][0]
            loaded = max(start for start in raw if start <= first + a)
            source = raw[loaded][:, :, first - loaded + a : first - loaded + b]
            copy(out=woven[i][:, a:b, :].rearrange("p (c i) t -> p c t i", i=4),
                 in_=source.rearrange("p t (c i) -> p c t i", i=4))

        def quantise(i):
            a, b = spans[i]
            nc.vector.quantize_mx(out=codes[:, a:b].bitcast(E5M2), scales=scales[:, a:b],
                                  in_=woven[i][:].rearrange("p c t -> p (c t)"))

        def product(nb, a, b, bank):
            acc = psum.tile([P, BANK], F32, name=f"acc{nb}_{a}", tag=f"bank{bank}")
            cols = slice(nb * P, (nb + 1) * P)
            start = a
            while start < b:
                width = max(w for w in (128, 256, 512) if w <= b - start)
                tokens = slice(start, start + width)
                part = acc[:, start - a : start - a + width]
                tiers = [(w4[:, 2 * nb * P : 2 * (nb + 1) * P].bitcast(E2M1), s4[:, cols]),
                         (w8[:, cols].bitcast(E4M3), s8[:, cols])]
                for i, (words, plane) in enumerate(reversed(tiers) if nb == 0 and a < 256 else tiers):
                    nc.tensor.matmul_mx(out=part, lhsT=words, lhsT_scale=plane, rhs=codes[:, tokens].bitcast(E5M2),
                                        rhs_scale=scales[:, tokens], start=i == 0, stop=i == 1)
                start += width
            return acc[:, : b - a]

        def window(nb, a, b):
            return pages[nb % 3][:].indirect(offsets[:, a // 16 : b // 16])

        def empty(nb, a, b, bank, over=None, slot=0, step=BANK):
            if over is None:
                dx[nb, a] = keep.tile([P, b - a], F32, name=f"dx{nb}_{a}")
            else:
                dx[nb, a] = shared.tile([P, b - a], F32, name=f"dx{nb}_{a}", align_bytes=64, offset=16 * over + 1024 * slot)
            for i, first in enumerate(range(a, b, step)):
                last = min(b, first + step)
                nc.scalar.copy(out=dx[nb, a][:, first - a : last - a], in_=product(nb, first, last, bank + i))

        def scatter(nb, a, b):
            nc.vector.tensor_tensor(out=window(nb, a, b), in0=dx[nb, a][:], in1=gain[:, a:b], op=mult)

        def store(nb):
            nc.sync.dma_start(out[nb * P : (nb + 1) * P, :], pages[nb % 3][:])

        nc.vector.memset(planes[:].bitcast(I32), 0)
        load_dy(0)
        load_weights(0, P)
        load_repeated_scale_rows(0, 2 * P)
        for plane, rows in ((s8, w8_scales), (s4, w4_scales)):
            nc.scalar.dma_start(plane[98:100, :].bitcast(I32), rows[0, REPEATED_ROWS:, :].bitcast(I32))
        load_gain(0, 256)
        nc.sync.dma_start(offsets[:], offs)
        load_weights(P, N)
        load_dy(1)
        load_repeated_scale_rows(2 * P, N)
        load_dy(2)
        load_gain(256, 512)
        load_dy(3)
        load_gain(512, J)

        for page in pages:
            nc.vector.memset(page[:].bitcast(I32), 0)
        for i in range(2):
            weave(nc.vector.tensor_copy, i, 0, VECTOR_SHARE)
            weave(nc.scalar.copy, i, VECTOR_SHARE, P)
        quantise(0)
        quantise(1)
        pages.append(shared.tile([P, T], F32, name="page2", align_bytes=64, offset=AT_PAGE2))
        nc.vector.memset(pages[2][:].bitcast(I32), 0)
        empty(0, 0, 256, 0, step=P)
        empty(1, 0, 256, 2)
        scatter(0, 0, 256)
        weave(nc.scalar.copy, 2, 0, 256)
        empty(2, 0, 256, 3, over=256)
        scatter(1, 0, 256)
        quantise(2)
        scatter(2, 0, 256)
        empty(0, 256, 512, 3)
        weave(nc.scalar.copy, 3, 0, 256)
        weave(nc.scalar.copy, 3, 256, 512)
        scatter(0, 256, 512)
        empty(1, 256, 512, 3, over=768)
        empty(2, 256, 512, 3, over=768, slot=1)
        quantise(3)
        scatter(1, 256, 512)
        scatter(2, 256, 512)
        for nb, first, bank in ((0, 512, 5), (1, 512, 6), (2, 512, 7), (3, 0, 3)):
            empty(nb, first, J, bank)
            scatter(nb, first, J)
            store(nb)
